import numpy as np
import ml_dtypes


def mxq(x, axis, fmt="e4m3"):
    dtype, down = {"e4m3": (ml_dtypes.float8_e4m3fn, 7), "e5m2": (ml_dtypes.float8_e5m2, 14)}[fmt]
    v = np.moveaxis(np.asarray(x, np.float32).astype(ml_dtypes.bfloat16).astype(np.float64), axis, -1)
    blocks = v.reshape(v.shape[:-1] + (-1, 32))
    amax = np.abs(blocks).max(-1, keepdims=True)
    byte = np.maximum(np.where(amax > 0, np.frexp(amax)[1] - 1 + 127, 0) - down, 1)
    scale = np.exp2(byte - 127.0)
    codes = (blocks / scale).astype(np.float32).astype(dtype).astype(np.float64)
    return np.moveaxis((codes * scale).reshape(v.shape), -1, axis)


WIDE = False


def mx_kscale(k):
    if not WIDE:
        return np.ones(k)
    levels = np.array([10, -10, 5, -5, 0])
    if k % 512:
        return np.exp2(np.random.permutation(np.resize(levels, k // 32))).repeat(32)
    a = np.empty((k // 512, 16))
    for p in range(k // 512):
        a[p, :8] = np.random.permutation(np.resize(levels, 8))
        for g in range(8):
            far = levels[np.abs(levels - a[p, g]) >= 10]
            a[p, g + 8] = far[np.random.randint(len(far))]
    return np.exp2(a.ravel()).repeat(32)


def f64(x):
    return np.asarray(x).astype(np.float64)


def striped(idx):
    return np.tile(idx.reshape(-1, 16).T, (8, 1)).astype(np.uint16)


def unstriped(offs):
    return offs[:16].T.reshape(-1).astype(np.int64)


def striped8(idx):
    return np.concatenate([x.reshape(-1, 16).T for x in idx]).astype(np.uint16)


def runs(offs, k):
    lists = np.stack([offs[16 * r : 16 * r + 16].T.reshape(-1) for r in range(8)]).astype(np.int64)
    return lists[np.arange(k) % 512 // 64]


def pack_weight(w):
    k, n = w.shape
    w = f64(np.asarray(w, np.float32).astype(ml_dtypes.bfloat16)).reshape(k // 32, 32, n)
    amax = np.abs(w).max(1)
    byte = np.clip(np.where(amax > 0, np.frexp(amax)[1] - 1 + 127 - 7, 1), 1, 254)
    scaled = (w * np.exp2(127.0 - byte)[:, None, :]).reshape(k, n).astype(np.float32)
    words = np.ascontiguousarray(scaled.reshape(k // 512, 128, 4, n).transpose(0, 1, 3, 2)).astype(ml_dtypes.float8_e4m3fn).view(np.uint8)
    return words, np.ascontiguousarray(byte.astype(np.uint8).reshape(k // 512, 16, n))


def unpack_weight(words, scales):
    g, p, n, _ = words.shape
    vals = np.ascontiguousarray(words).view(ml_dtypes.float8_e4m3fn).astype(np.float64) * np.repeat(np.exp2(scales.astype(np.float64) - 127.0), 8, axis=1)[..., None]
    return vals.transpose(0, 1, 3, 2).reshape(g * 512, n)


def sigmoid(v):
    return 1.0 / (1.0 + np.exp(-np.maximum(v, -700.0)))

def planes(y):
    n, m = y.shape
    v = y.astype(np.float32).astype(ml_dtypes.bfloat16).astype(np.float64).reshape(n // 32, 32, m)
    top = np.abs(v).max(1)
    byte = np.clip(np.where(top > 0, np.frexp(top)[1] - 1 + 127 - 7, 1), 1, 254)
    codes = (v * np.exp2(127.0 - byte)[:, None, :]).reshape(n, m).astype(np.float32).astype(ml_dtypes.float8_e4m3fn).view(np.uint8)
    words = codes.reshape(n // 512, 128, 4, m).transpose(0, 1, 3, 2)
    return np.ascontiguousarray(words), np.ascontiguousarray(byte.astype(np.uint8).reshape(n // 512, 16, m))


K, T, S, N, G, H, U = 512, 2048, 512, 512, 2048, 512, 1024


def setup_inputs():
    n = np.random.standard_normal
    s = mx_kscale(K)[:, None]
    u = mx_kscale(H)
    packed_xT = pack_weight(n((K, T)) * s)
    packed_dT = pack_weight(n((K, G)) / s)
    packed_w1 = pack_weight(n((H, N)) / np.sqrt(H) / u[:, None])
    return {
        "x_words": packed_xT[0],
        "x_scales": packed_xT[1],
        "d_words": packed_dT[0],
        "d_scales": packed_dT[1],
        "tab": n((H, U)).astype(np.float32),
        "gn": (np.random.uniform(0.5, 1.5, (H, 1)) * u[:, None]).astype(np.float32),
        "w1_words": packed_w1[0],
        "w1_scales": packed_w1[1],
        "offs": striped(np.random.permutation(T)[:S]),
        "kidx": striped8(np.random.randint(0, G, (8, H))),
        "rel": striped8(np.random.randint(0, U, (8, S))),
    }


def reference(x_words, x_scales, d_words, d_scales, tab, gn, w1_words, w1_scales, offs, kidx, rel):
    d_kidx = unpack_weight(d_words, d_scales)[np.arange(K)[:, None], runs(kidx, K)]
    xq = unpack_weight(x_words, x_scales)[:, unstriped(offs)]
    s = 0.0625 * (d_kidx.T @ xq)
    z = f64(gn) * (sigmoid(s + f64(tab)[np.arange(H)[:, None], runs(rel, H)]))
    out_0 = unpack_weight(w1_words, w1_scales).T @ mxq(z, 0, "e4m3")
    return (out_0,) + planes(out_0)

@@ -1,0 +1,210 @@
+from contextlib import ExitStack
+
+import concourse.mybir as mybir
+
+K, T, S, N, G, H, U = 512, 2048, 512, 512, 2048, 512, 1024
+FLOPS = 2 * K * H * S + 2 * H * N * S
+
+F32 = mybir.dt.float32
+BF16 = mybir.dt.bfloat16
+I32 = mybir.dt.int32
+U32 = mybir.dt.uint32
+U16 = mybir.dt.uint16
+U8 = mybir.dt.uint8
+FP8X4 = mybir.dt.float8_e4m3fn_x4
+ACT = mybir.ActivationFunctionType
+ALU = mybir.AluOpType
+
+P = 128
+PACK = 4
+HALF = 256
+CHUNK = 128
+
+
+def words_of(dram):
+    return dram[0].rearrange("p n r -> p (n r)").bitcast(I32)
+
+
+def deal(nc, dst, src):
+    nc.vector.tensor_copy(dst.rearrange("p (t m) -> p t m", t=PACK), src.rearrange("p (m t) -> p t m", t=PACK))
+
+
+def tile_picked_scorebias_sigmoid_po_kernel(
+    tc, x_words, x_scales, d_words, d_scales, tab, gn, w1_words, w1_scales, offs, kidx, rel, out_0, out_1, out_2
+):
+    nc = tc.nc
+    with ExitStack() as ctx:
+        keep = ctx.enter_context(tc.tile_pool(name="keep", bufs=1))
+        psum = ctx.enter_context(tc.psum_pool(name="psum", bufs=1))
+
+        def sb(shape, dtype, name, tag=None):
+            return keep.tile(shape, dtype, name=name, tag=tag or name, align_bytes=64)
+
+        kidx_t = keep.tile([P, H // 16], U16, name="kidx_t")
+        offs_t = keep.tile([P, S // 16], U16, name="offs_t")
+        rel_t = keep.tile([P, S // 16], U16, name="rel_t")
+        d_sc_win = sb([P, G], U8, "d_sc_win")
+        x_sc_win = sb([P, T], U8, "x_sc_win", "tab1")
+        w_sc_raw = sb([P, N], U8, "w_sc_raw")
+        d_win = sb([P, G], U32, "d_win", "tab2")
+        x_win = sb([P, T], U32, "x_win", "w_raw")
+        gn_t = sb([P, PACK], F32, "gn_t")
+        warm = sb([P, 2], F32, "warm")
+
+        tab_rows = tab.rearrange("(p t) u -> p t u", t=PACK)
+        tab_t = []
+
+        def load_tab(t):
+            tile = sb([P, U], F32, "tab%d" % t)
+            nc.sync.dma_start(tile[:], tab_rows[:, t, :])
+            tab_t.append(tile)
+
+        nc.vector.memset(d_sc_win[:, : G // 2].bitcast(I32), 0)
+        nc.gpsimd.memset(d_sc_win[:, G // 2 :].bitcast(I32), 0)
+        nc.vector.memset(x_sc_win[:].bitcast(I32), 0)
+        nc.vector.memset(warm[:, 0:1], 0.0)
+        nc.gpsimd.memset(w_sc_raw[:].bitcast(I32), 0)
+
+        nc.sync.dma_start(kidx_t[:], kidx)
+        nc.sync.dma_start(offs_t[:], offs)
+        nc.sync.dma_start(rel_t[:], rel)
+        for e in range(2):
+            nc.sync.dma_start(d_sc_win[e:P:16, :].bitcast(I32), d_scales[0, e:16:2, :].bitcast(I32))
+        nc.sync.dma_start(d_win[:].bitcast(I32), words_of(d_words))
+        nc.sync.dma_start(x_win[:].bitcast(I32), words_of(x_words))
+        for q in range(4):
+            nc.scalar.dma_start(x_sc_win[32 * q : 32 * q + 4, :].bitcast(I32), x_scales[0, 4 * q : 4 * q + 4, :].bitcast(I32))
+        nc.scalar.activation(warm[:, 1:2], warm[:, 0:1], ACT.Sigmoid)
+        for q in range(4):
+            nc.gpsimd.dma_start(w_sc_raw[32 * q : 32 * q + 4, :].bitcast(I32), w1_scales[0, 4 * q : 4 * q + 4, :].bitcast(I32))
+        nc.gpsimd.dma_start(gn_t[:], gn.rearrange("(p t) o -> p (t o)", t=PACK))
+
+        d_sc_got = sb([P, H], U8, "d_sc_got", "tab0")
+        d_sc = sb([P, H], U8, "d_sc")
+        nc.vector.tensor_copy(d_sc_got[:], d_sc_win[:].indirect(kidx_t[:]))
+        deal(nc, d_sc[:], d_sc_got[:])
+        for e in range(2):
+            nc.sync.dma_start(d_sc[2 + e : P : 32, :].bitcast(I32), d_sc[16 + e : P : 32, :].bitcast(I32))
+        load_tab(0)
+        x_sc = sb([P, S], U8, "x_sc")
+        nc.vector.tensor_copy(x_sc[:], x_sc_win[:].indirect(offs_t[:]))
+        load_tab(1)
+        d_got = sb([P, H], U32, "d_got", "tab3")
+        d_q = sb([P, H], U32, "d_q")
+        nc.vector.tensor_copy(d_got[:], d_win[:].indirect(kidx_t[:]))
+        load_tab(2)
+        deal(nc, d_q[:].bitcast(I32), d_got[:].bitcast(I32))
+        load_tab(3)
+
+        halves = range(S // HALF)
+        score = {}
+        for h in halves:
+            x_q = sb([P, HALF], U32, "x_q%d" % h)
+            nc.vector.tensor_copy(x_q[:], x_win[:].indirect(offs_t[:, h * 16 : (h + 1) * 16]))
+            for a in range(2):
+                bank = psum.tile([P, 2, HALF], F32, name="s_bank%d%d" % (h, a))
+                for b in range(2):
+                    cols = slice((2 * a + b) * P, (2 * a + b + 1) * P)
+                    nc.tensor.matmul_mx(
+                        out=bank[:, b, :],
+                        lhsT=d_q[:, cols].bitcast(FP8X4),
+                        lhsT_scale=d_sc[:, cols],
+                        rhs=x_q[:].bitcast(FP8X4),
+                        rhs_scale=x_sc[:, h * HALF : (h + 1) * HALF],
+                        start=True,
+                        stop=True,
+                    )
+                sc = sb([P, 2, HALF], F32, "score%d%d" % (h, a))
+                nc.scalar.activation(sc[:], bank[:], ACT.Copy, scale=0.0625)
+                score[(h, a)] = sc
+
+        w_raw = sb([P, N], U32, "w_raw")
+        nc.sync.dma_start(w_raw[:].bitcast(I32), words_of(w1_words))
+        w_sc = sb([P, N], U8, "w_sc", "x_q0")
+        deal(nc, w_sc[:], w_sc_raw[:])
+        w_q = sb([P, N], U32, "w_q")
+
+        sig = [sb([P, PACK, HALF], F32, "sig%d" % h) for h in halves]
+
+        def sigmoids(t, h):
+            u = sb([P, HALF], F32, "u%d%d" % (t, h))
+            nc.vector.tensor_tensor(
+                u[:], tab_t[t][:].indirect(rel_t[:, h * 16 : (h + 1) * 16]), score[(h, t // 2)][:, t % 2, :], ALU.add
+            )
+            nc.scalar.activation(sig[h][:, t, :], u[:], ACT.Sigmoid)
+
+        y_words = [sb([P, HALF], U32, "y_words%d" % h) for h in halves]
+        y_sc = sb([P, S], U8, "y_sc")
+        out_rows = out_0.rearrange("(p t) j -> p t j", t=PACK)
+        gn_b = gn_t[:].unsqueeze(1).unsqueeze(3).to_broadcast([P, CHUNK // 4, PACK, 4])
+        zs, ys, banks = {}, {}, {}
+
+        def weigh(c):
+            h, lo = divmod(c * CHUNK, HALF)
+            z = sb([P, CHUNK * PACK], BF16, "z%d" % c)
+            nc.vector.tensor_tensor(
+                z[:].rearrange("p (g i t) -> p g t i", i=4, t=PACK),
+                sig[h][:, :, lo : lo + CHUNK].rearrange("p t (g i) -> p g t i", i=4),
+                gn_b,
+                ALU.mult,
+            )
+            zs[c] = z
+
+        def product(c):
+            z_q = sb([P, CHUNK], U32, "z_q%d" % c)
+            z_sc = sb([P, CHUNK], U8, "z_sc%d" % c)
+            nc.vector.quantize_mx(out=z_q[:].bitcast(FP8X4), scales=z_sc[:], in_=zs[c][:])
+            bank = psum.tile([P, PACK, CHUNK], F32, name="y_bank%d" % c)
+            for t in range(PACK):
+                wc = slice(t * P, (t + 1) * P)
+                nc.tensor.matmul_mx(
+                    out=bank[:, t, :],
+                    lhsT=w_q[:, wc].bitcast(FP8X4),
+                    lhsT_scale=w_sc[:, wc],
+                    rhs=z_q[:].bitcast(FP8X4),
+                    rhs_scale=z_sc[:],
+                    start=True,
+                    stop=True,
+                )
+            y = sb([P, PACK, CHUNK], F32, "y%d" % c)
+            nc.scalar.copy(y[:], bank[:])
+            nc.sync.dma_start(out_rows[:, :, c * CHUNK : (c + 1) * CHUNK], y[:])
+            ys[c], banks[c] = y, bank
+
+        def planes(c):
+            h, lo = divmod(c * CHUNK, HALF)
+            yb = sb([P, CHUNK * PACK], BF16, "yb%d" % c)
+            yb_v = yb[:].rearrange("p (g i t) -> p g t i", i=4, t=PACK)
+            if c < 2:
+                nc.scalar.copy(yb_v, banks[c][:].rearrange("p t (g i) -> p g t i", i=4))
+            else:
+                nc.vector.tensor_copy(yb_v, ys[c][:].rearrange("p t (g i) -> p g t i", i=4))
+            nc.vector.quantize_mx(
+                out=y_words[h][:, lo : lo + CHUNK].bitcast(FP8X4), scales=y_sc[:, c * CHUNK : (c + 1) * CHUNK], in_=yb[:]
+            )
+
+        def store_words(h):
+            nc.sync.dma_start(words_of(out_1)[:, h * HALF : (h + 1) * HALF], y_words[h][:].bitcast(I32))
+
+        for t, h in ((0, 0), (0, 1), (1, 0), (1, 1), (2, 0), (3, 0)):
+            sigmoids(t, h)
+        deal(nc, w_q[:].bitcast(I32), w_raw[:].bitcast(I32))
+        sigmoids(2, 1)
+        weigh(0)
+        weigh(1)
+        product(0)
+        product(1)
+        sigmoids(3, 1)
+        planes(0)
+        weigh(2)
+        planes(1)
+        store_words(0)
+        weigh(3)
+        product(2)
+        product(3)
+        planes(2)
+        planes(3)
+        store_words(1)
+        for q in range(4):
+            eng = nc.sync if q % 2 else nc.scalar
+            eng.dma_start(out_2[0, 4 * q : 4 * q + 4, :].bitcast(I32), y_sc[32 * q : 32 * q + 4, :].bitcast(I32))

@@ -26,7 +26,9 @@ def words_of(dram):
 
 
 def deal(nc, dst, src):
-    nc.vector.tensor_copy(dst.rearrange("p (t m) -> p t m", t=PACK), src.rearrange("p (m t) -> p t m", t=PACK))
+    nc.vector.tensor_copy(
+        dst.rearrange("p (t g i) -> p g t i", t=PACK, i=4), src.rearrange("p (g i t) -> p g t i", t=PACK, i=4)
+    )
 
 
 def tile_picked_scorebias_sigmoid_po_kernel(
@@ -44,11 +46,9 @@ def tile_picked_scorebias_sigmoid_po_kernel(
         offs_t = keep.tile([P, S // 16], U16, name="offs_t")
         rel_t = keep.tile([P, S // 16], U16, name="rel_t")
         d_sc_win = sb([P, G], U8, "d_sc_win")
-        x_sc_win = sb([P, T], U8, "x_sc_win", "tab1")
-        w_sc_raw = sb([P, N], U8, "w_sc_raw")
-        d_win = sb([P, G], U32, "d_win", "tab2")
+        x_sc_win = sb([P, T], U8, "x_sc_win", "tab3")
+        d_win = sb([P, G], U32, "d_win", "tab1")
         x_win = sb([P, T], U32, "x_win", "w_raw")
-        gn_t = sb([P, PACK], F32, "gn_t")
         warm = sb([P, 2], F32, "warm")
 
         tab_rows = tab.rearrange("(p t) u -> p t u", t=PACK)
@@ -61,39 +61,37 @@ def tile_picked_scorebias_sigmoid_po_kernel(
 
         nc.vector.memset(d_sc_win[:, : G // 2].bitcast(I32), 0)
         nc.gpsimd.memset(d_sc_win[:, G // 2 :].bitcast(I32), 0)
-        nc.vector.memset(x_sc_win[:].bitcast(I32), 0)
         nc.vector.memset(warm[:, 0:1], 0.0)
-        nc.gpsimd.memset(w_sc_raw[:].bitcast(I32), 0)
+        nc.vector.memset(x_sc_win[:].bitcast(I32), 0)
 
         nc.sync.dma_start(kidx_t[:], kidx)
         nc.sync.dma_start(offs_t[:], offs)
-        nc.sync.dma_start(rel_t[:], rel)
         for e in range(2):
             nc.sync.dma_start(d_sc_win[e:P:16, :].bitcast(I32), d_scales[0, e:16:2, :].bitcast(I32))
         nc.sync.dma_start(d_win[:].bitcast(I32), words_of(d_words))
+        nc.sync.dma_start(rel_t[:], rel)
         nc.sync.dma_start(x_win[:].bitcast(I32), words_of(x_words))
-        for q in range(4):
-            nc.scalar.dma_start(x_sc_win[32 * q : 32 * q + 4, :].bitcast(I32), x_scales[0, 4 * q : 4 * q + 4, :].bitcast(I32))
+        load_tab(0)
         nc.scalar.activation(warm[:, 1:2], warm[:, 0:1], ACT.Sigmoid)
         for q in range(4):
-            nc.gpsimd.dma_start(w_sc_raw[32 * q : 32 * q + 4, :].bitcast(I32), w1_scales[0, 4 * q : 4 * q + 4, :].bitcast(I32))
-        nc.gpsimd.dma_start(gn_t[:], gn.rearrange("(p t) o -> p (t o)", t=PACK))
+            nc.scalar.dma_start(x_sc_win[32 * q : 32 * q + 4, :].bitcast(I32), x_scales[0, 4 * q : 4 * q + 4, :].bitcast(I32))
 
-        d_sc_got = sb([P, H], U8, "d_sc_got", "tab0")
+        d_sc_got = sb([P, H], U8, "d_sc_got")
         d_sc = sb([P, H], U8, "d_sc")
+        d_sc_odd = sb([P, H], U8, "d_sc_odd")
         nc.vector.tensor_copy(d_sc_got[:], d_sc_win[:].indirect(kidx_t[:]))
         deal(nc, d_sc[:], d_sc_got[:])
+        deal(nc, d_sc_odd[:], d_sc_got[:])
         for e in range(2):
-            nc.sync.dma_start(d_sc[2 + e : P : 32, :].bitcast(I32), d_sc[16 + e : P : 32, :].bitcast(I32))
-        load_tab(0)
-        x_sc = sb([P, S], U8, "x_sc")
-        nc.vector.tensor_copy(x_sc[:], x_sc_win[:].indirect(offs_t[:]))
-        load_tab(1)
-        d_got = sb([P, H], U32, "d_got", "tab3")
+            nc.scalar.dma_start(d_sc[2 + e : P : 32, :].bitcast(I32), d_sc_odd[16 + e : P : 32, :].bitcast(I32))
+        d_got = sb([P, H], U32, "d_got", "tab2")
         d_q = sb([P, H], U32, "d_q")
         nc.vector.tensor_copy(d_got[:], d_win[:].indirect(kidx_t[:]))
-        load_tab(2)
+        load_tab(1)
         deal(nc, d_q[:].bitcast(I32), d_got[:].bitcast(I32))
+        load_tab(2)
+        x_sc = sb([P, S], U8, "x_sc")
+        nc.vector.tensor_copy(x_sc[:], x_sc_win[:].indirect(offs_t[:]))
         load_tab(3)
 
         halves = range(S // HALF)
@@ -120,8 +118,13 @@ def tile_picked_scorebias_sigmoid_po_kernel(
 
         w_raw = sb([P, N], U32, "w_raw")
         nc.sync.dma_start(w_raw[:].bitcast(I32), words_of(w1_words))
-        w_sc = sb([P, N], U8, "w_sc", "x_q0")
-        deal(nc, w_sc[:], w_sc_raw[:])
+        w_sc_raw = sb([P, N], U8, "w_sc_raw", "x_q0")
+        nc.vector.memset(w_sc_raw[:].bitcast(I32), 0)
+        for q in range(4):
+            nc.sync.dma_start(w_sc_raw[32 * q : 32 * q + 4, :].bitcast(I32), w1_scales[0, 4 * q : 4 * q + 4, :].bitcast(I32))
+        w_sc = sb([P, N], U8, "w_sc")
+        gn_t = sb([P, PACK], F32, "gn_t", "x_q1")
+        nc.sync.dma_start(gn_t[:], gn.rearrange("(p t) o -> p (t o)", t=PACK))
         w_q = sb([P, N], U32, "w_q")
 
         sig = [sb([P, PACK, HALF], F32, "sig%d" % h) for h in halves]
@@ -166,21 +169,22 @@ def tile_picked_scorebias_sigmoid_po_kernel(
                     start=True,
                     stop=True,
                 )
+            banks[c] = bank
+
+        def store_floats(c):
             y = sb([P, PACK, CHUNK], F32, "y%d" % c)
-            nc.scalar.copy(y[:], bank[:])
+            nc.scalar.copy(y[:], banks[c][:])
             nc.sync.dma_start(out_rows[:, :, c * CHUNK : (c + 1) * CHUNK], y[:])
-            ys[c], banks[c] = y, bank
+
+        def round_result(c, copy):
+            yb = sb([P, CHUNK * PACK], BF16, "yb%d" % c)
+            copy(yb[:].rearrange("p (g i t) -> p g t i", i=4, t=PACK), banks[c][:].rearrange("p t (g i) -> p g t i", i=4))
+            ys[c] = yb
 
         def planes(c):
             h, lo = divmod(c * CHUNK, HALF)
-            yb = sb([P, CHUNK * PACK], BF16, "yb%d" % c)
-            yb_v = yb[:].rearrange("p (g i t) -> p g t i", i=4, t=PACK)
-            if c < 2:
-                nc.scalar.copy(yb_v, banks[c][:].rearrange("p t (g i) -> p g t i", i=4))
-            else:
-                nc.vector.tensor_copy(yb_v, ys[c][:].rearrange("p t (g i) -> p g t i", i=4))
             nc.vector.quantize_mx(
-                out=y_words[h][:, lo : lo + CHUNK].bitcast(FP8X4), scales=y_sc[:, c * CHUNK : (c + 1) * CHUNK], in_=yb[:]
+                out=y_words[h][:, lo : lo + CHUNK].bitcast(FP8X4), scales=y_sc[:, c * CHUNK : (c + 1) * CHUNK], in_=ys[c][:]
             )
 
         def store_words(h):
@@ -189,19 +193,27 @@ def tile_picked_scorebias_sigmoid_po_kernel(
         for t, h in ((0, 0), (0, 1), (1, 0), (1, 1), (2, 0), (3, 0)):
             sigmoids(t, h)
         deal(nc, w_q[:].bitcast(I32), w_raw[:].bitcast(I32))
+        deal(nc, w_sc[:], w_sc_raw[:])
         sigmoids(2, 1)
         weigh(0)
         weigh(1)
         product(0)
         product(1)
         sigmoids(3, 1)
-        planes(0)
+        for c in (0, 1):
+            store_floats(c)
+            round_result(c, nc.scalar.copy)
         weigh(2)
-        planes(1)
-        store_words(0)
         weigh(3)
         product(2)
         product(3)
+        planes(0)
+        planes(1)
+        store_words(0)
+        round_result(2, nc.scalar.copy)
+        round_result(3, nc.vector.tensor_copy)
+        store_floats(2)
+        store_floats(3)
         planes(2)
         planes(3)
         store_words(1)

@@ -18,7 +18,7 @@ ALU = mybir.AluOpType
 P = 128
 PACK = 4
 HALF = 256
-CHUNK = 128
+CHUNKS = ((0, 128), (128, 128), (256, 128), (384, 128))
 
 
 def words_of(dram):
@@ -42,14 +42,17 @@ def tile_picked_scorebias_sigmoid_po_kernel(
         def sb(shape, dtype, name, tag=None):
             return keep.tile(shape, dtype, name=name, tag=tag or name, align_bytes=64)
 
+        def load_scale_rows(queue, plane, dram):
+            for q in range(4):
+                queue.dma_start(plane[32 * q : 32 * q + 4, :].bitcast(I32), dram[0, 4 * q : 4 * q + 4, :].bitcast(I32))
+
         kidx_t = keep.tile([P, H // 16], U16, name="kidx_t")
         offs_t = keep.tile([P, S // 16], U16, name="offs_t")
         rel_t = keep.tile([P, S // 16], U16, name="rel_t")
         d_sc_win = sb([P, G], U8, "d_sc_win")
-        x_sc_win = sb([P, T], U8, "x_sc_win", "tab3")
+        x_sc_win = sb([P, T], U8, "x_sc_win", "tab2")
         d_win = sb([P, G], U32, "d_win", "tab1")
         x_win = sb([P, T], U32, "x_win", "w_raw")
-        warm = sb([P, 2], F32, "warm")
 
         tab_rows = tab.rearrange("(p t) u -> p t u", t=PACK)
         tab_t = []
@@ -59,55 +62,60 @@ def tile_picked_scorebias_sigmoid_po_kernel(
             nc.sync.dma_start(tile[:], tab_rows[:, t, :])
             tab_t.append(tile)
 
-        nc.vector.memset(d_sc_win[:, : G // 2].bitcast(I32), 0)
-        nc.gpsimd.memset(d_sc_win[:, G // 2 :].bitcast(I32), 0)
-        nc.vector.memset(warm[:, 0:1], 0.0)
-        nc.vector.memset(x_sc_win[:].bitcast(I32), 0)
+        for win in (d_sc_win, x_sc_win):
+            nc.vector.memset(win[:, : G // 2].bitcast(I32), 0)
+            nc.gpsimd.memset(win[:, G // 2 :].bitcast(I32), 0)
 
         nc.sync.dma_start(kidx_t[:], kidx)
         nc.sync.dma_start(offs_t[:], offs)
         for e in range(2):
             nc.sync.dma_start(d_sc_win[e:P:16, :].bitcast(I32), d_scales[0, e:16:2, :].bitcast(I32))
         nc.sync.dma_start(d_win[:].bitcast(I32), words_of(d_words))
-        nc.sync.dma_start(rel_t[:], rel)
+        load_scale_rows(nc.sync, x_sc_win, x_scales)
         nc.sync.dma_start(x_win[:].bitcast(I32), words_of(x_words))
-        load_tab(0)
-        nc.scalar.activation(warm[:, 1:2], warm[:, 0:1], ACT.Sigmoid)
-        for q in range(4):
-            nc.scalar.dma_start(x_sc_win[32 * q : 32 * q + 4, :].bitcast(I32), x_scales[0, 4 * q : 4 * q + 4, :].bitcast(I32))
+        nc.sync.dma_start(rel_t[:], rel)
 
-        d_sc_got = sb([P, H], U8, "d_sc_got")
+        d_sc_got = sb([P, H], U8, "d_sc_got", "tab0")
         d_sc = sb([P, H], U8, "d_sc")
-        d_sc_odd = sb([P, H], U8, "d_sc_odd")
         nc.vector.tensor_copy(d_sc_got[:], d_sc_win[:].indirect(kidx_t[:]))
-        deal(nc, d_sc[:], d_sc_got[:])
-        deal(nc, d_sc_odd[:], d_sc_got[:])
-        for e in range(2):
-            nc.scalar.dma_start(d_sc[2 + e : P : 32, :].bitcast(I32), d_sc_odd[16 + e : P : 32, :].bitcast(I32))
-        d_got = sb([P, H], U32, "d_got", "tab2")
+        d_sc_dealt = sb([P, H], U8, "d_sc_dealt")
+        deal(nc, d_sc_dealt[:], d_sc_got[:])
+        for r in range(4):
+            src = 16 * (r // 2) + r % 2
+            nc.scalar.dma_start(d_sc[r:P:32, :].bitcast(I32), d_sc_dealt[src:P:32, :].bitcast(I32))
+        load_tab(0)
+
+        d_got = sb([P, H], U32, "d_got", "tab3")
         d_q = sb([P, H], U32, "d_q")
         nc.vector.tensor_copy(d_got[:], d_win[:].indirect(kidx_t[:]))
         load_tab(1)
-        deal(nc, d_q[:].bitcast(I32), d_got[:].bitcast(I32))
-        load_tab(2)
+
         x_sc = sb([P, S], U8, "x_sc")
         nc.vector.tensor_copy(x_sc[:], x_sc_win[:].indirect(offs_t[:]))
+        load_tab(2)
+        deal(nc, d_q[:].bitcast(I32), d_got[:].bitcast(I32))
         load_tab(3)
 
         halves = range(S // HALF)
-        score = {}
+        x_q = []
         for h in halves:
-            x_q = sb([P, HALF], U32, "x_q%d" % h)
-            nc.vector.tensor_copy(x_q[:], x_win[:].indirect(offs_t[:, h * 16 : (h + 1) * 16]))
-            for a in range(2):
-                bank = psum.tile([P, 2, HALF], F32, name="s_bank%d%d" % (h, a))
+            x_q.append(sb([P, HALF], U32, "x_q%d" % h))
+            nc.vector.tensor_copy(x_q[h][:], x_win[:].indirect(offs_t[:, h * 16 : (h + 1) * 16]))
+        w_raw = sb([P, N], U32, "w_raw")
+        nc.sync.dma_start(w_raw[:].bitcast(I32), words_of(w1_words))
+        w_q = sb([P, N], U32, "w_q")
+
+        score = {}
+        for a in range(2):
+            for h in halves:
+                bank = psum.tile([P, 2, HALF], F32, name="s_bank%d%d" % (h, a), tag="bank%d" % (2 * a + h))
                 for b in range(2):
                     cols = slice((2 * a + b) * P, (2 * a + b + 1) * P)
                     nc.tensor.matmul_mx(
                         out=bank[:, b, :],
                         lhsT=d_q[:, cols].bitcast(FP8X4),
                         lhsT_scale=d_sc[:, cols],
-                        rhs=x_q[:].bitcast(FP8X4),
+                        rhs=x_q[h][:].bitcast(FP8X4),
                         rhs_scale=x_sc[:, h * HALF : (h + 1) * HALF],
                         start=True,
                         stop=True,
@@ -115,17 +123,12 @@ def tile_picked_scorebias_sigmoid_po_kernel(
                 sc = sb([P, 2, HALF], F32, "score%d%d" % (h, a))
                 nc.scalar.activation(sc[:], bank[:], ACT.Copy, scale=0.0625)
                 score[(h, a)] = sc
-
-        w_raw = sb([P, N], U32, "w_raw")
-        nc.sync.dma_start(w_raw[:].bitcast(I32), words_of(w1_words))
         w_sc_raw = sb([P, N], U8, "w_sc_raw", "x_q0")
         nc.vector.memset(w_sc_raw[:].bitcast(I32), 0)
-        for q in range(4):
-            nc.sync.dma_start(w_sc_raw[32 * q : 32 * q + 4, :].bitcast(I32), w1_scales[0, 4 * q : 4 * q + 4, :].bitcast(I32))
+        load_scale_rows(nc.sync, w_sc_raw, w1_scales)
         w_sc = sb([P, N], U8, "w_sc")
         gn_t = sb([P, PACK], F32, "gn_t", "x_q1")
         nc.sync.dma_start(gn_t[:], gn.rearrange("(p t) o -> p (t o)", t=PACK))
-        w_q = sb([P, N], U32, "w_q")
 
         sig = [sb([P, PACK, HALF], F32, "sig%d" % h) for h in halves]
 
@@ -139,25 +142,26 @@ def tile_picked_scorebias_sigmoid_po_kernel(
         y_words = [sb([P, HALF], U32, "y_words%d" % h) for h in halves]
         y_sc = sb([P, S], U8, "y_sc")
         out_rows = out_0.rearrange("(p t) j -> p t j", t=PACK)
-        gn_b = gn_t[:].unsqueeze(1).unsqueeze(3).to_broadcast([P, CHUNK // 4, PACK, 4])
         zs, ys, banks = {}, {}, {}
 
         def weigh(c):
-            h, lo = divmod(c * CHUNK, HALF)
-            z = sb([P, CHUNK * PACK], BF16, "z%d" % c)
+            j0, n = CHUNKS[c]
+            h, lo = divmod(j0, HALF)
+            z = sb([P, n * PACK], BF16, "z%d" % c)
             nc.vector.tensor_tensor(
                 z[:].rearrange("p (g i t) -> p g t i", i=4, t=PACK),
-                sig[h][:, :, lo : lo + CHUNK].rearrange("p t (g i) -> p g t i", i=4),
-                gn_b,
+                sig[h][:, :, lo : lo + n].rearrange("p t (g i) -> p g t i", i=4),
+                gn_t[:].unsqueeze(1).unsqueeze(3).to_broadcast([P, n // 4, PACK, 4]),
                 ALU.mult,
             )
             zs[c] = z
 
         def product(c):
-            z_q = sb([P, CHUNK], U32, "z_q%d" % c)
-            z_sc = sb([P, CHUNK], U8, "z_sc%d" % c)
+            n = CHUNKS[c][1]
+            z_q = sb([P, n], U32, "z_q%d" % c)
+            z_sc = sb([P, n], U8, "z_sc%d" % c)
             nc.vector.quantize_mx(out=z_q[:].bitcast(FP8X4), scales=z_sc[:], in_=zs[c][:])
-            bank = psum.tile([P, PACK, CHUNK], F32, name="y_bank%d" % c)
+            bank = psum.tile([P, PACK, n], F32, name="y_bank%d" % c, tag="bank%d" % ((4 + c) % 8))
             for t in range(PACK):
                 wc = slice(t * P, (t + 1) * P)
                 nc.tensor.matmul_mx(
@@ -172,25 +176,30 @@ def tile_picked_scorebias_sigmoid_po_kernel(
             banks[c] = bank
 
         def store_floats(c):
-            y = sb([P, PACK, CHUNK], F32, "y%d" % c)
+            j0, n = CHUNKS[c]
+            y = sb([P, PACK, n], F32, "y%d" % c)
             nc.scalar.copy(y[:], banks[c][:])
-            nc.sync.dma_start(out_rows[:, :, c * CHUNK : (c + 1) * CHUNK], y[:])
+            nc.sync.dma_start(out_rows[:, :, j0 : j0 + n], y[:])
 
         def round_result(c, copy):
-            yb = sb([P, CHUNK * PACK], BF16, "yb%d" % c)
-            copy(yb[:].rearrange("p (g i t) -> p g t i", i=4, t=PACK), banks[c][:].rearrange("p t (g i) -> p g t i", i=4))
+            n = CHUNKS[c][1]
+            yb = sb([P, n, PACK], BF16, "yb%d" % c)
+            copy(yb[:], banks[c][:].rearrange("p t j -> p j t"))
             ys[c] = yb
 
         def planes(c):
-            h, lo = divmod(c * CHUNK, HALF)
+            j0, n = CHUNKS[c]
+            h, lo = divmod(j0, HALF)
             nc.vector.quantize_mx(
-                out=y_words[h][:, lo : lo + CHUNK].bitcast(FP8X4), scales=y_sc[:, c * CHUNK : (c + 1) * CHUNK], in_=ys[c][:]
+                out=y_words[h][:, lo : lo + n].bitcast(FP8X4),
+                scales=y_sc[:, j0 : j0 + n],
+                in_=ys[c][:].rearrange("p j t -> p (j t)"),
             )
 
         def store_words(h):
             nc.sync.dma_start(words_of(out_1)[:, h * HALF : (h + 1) * HALF], y_words[h][:].bitcast(I32))
 
-        for t, h in ((0, 0), (0, 1), (1, 0), (1, 1), (2, 0), (3, 0)):
+        for t, h in ((0, 0), (1, 0), (0, 1), (1, 1), (2, 0), (3, 0)):
             sigmoids(t, h)
         deal(nc, w_q[:].bitcast(I32), w_raw[:].bitcast(I32))
         deal(nc, w_sc[:], w_sc_raw[:])

@@ -50,7 +50,7 @@ def tile_picked_scorebias_sigmoid_po_kernel(
         offs_t = keep.tile([P, S // 16], U16, name="offs_t")
         rel_t = keep.tile([P, S // 16], U16, name="rel_t")
         d_sc_win = sb([P, G], U8, "d_sc_win")
-        x_sc_win = sb([P, T], U8, "x_sc_win", "tab2")
+        x_sc_win = sb([P, T], U8, "x_sc_win", "tab0")
         d_win = sb([P, G], U32, "d_win", "tab1")
         x_win = sb([P, T], U32, "x_win", "w_raw")
 
@@ -65,35 +65,35 @@ def tile_picked_scorebias_sigmoid_po_kernel(
         for win in (d_sc_win, x_sc_win):
             nc.vector.memset(win[:, : G // 2].bitcast(I32), 0)
             nc.gpsimd.memset(win[:, G // 2 :].bitcast(I32), 0)
+        warm = sb([P, 2], F32, "warm")
+        nc.vector.memset(warm[:, 0:1], 0.0)
+        nc.scalar.activation(warm[:, 1:2], warm[:, 0:1], ACT.Sigmoid)
 
         nc.sync.dma_start(kidx_t[:], kidx)
         nc.sync.dma_start(offs_t[:], offs)
-        for e in range(2):
-            nc.sync.dma_start(d_sc_win[e:P:16, :].bitcast(I32), d_scales[0, e:16:2, :].bitcast(I32))
-        nc.sync.dma_start(d_win[:].bitcast(I32), words_of(d_words))
+        nc.sync.dma_start(d_sc_win[0:P:8, :].bitcast(I32), d_scales[0].bitcast(I32))
         load_scale_rows(nc.sync, x_sc_win, x_scales)
+        nc.sync.dma_start(d_win[:].bitcast(I32), words_of(d_words))
         nc.sync.dma_start(x_win[:].bitcast(I32), words_of(x_words))
         nc.sync.dma_start(rel_t[:], rel)
 
-        d_sc_got = sb([P, H], U8, "d_sc_got", "tab0")
+        d_sc_got = sb([P, H], U8, "d_sc_got")
+        d_sc_dealt = sb([P, H], U8, "d_sc_dealt", "tab3")
         d_sc = sb([P, H], U8, "d_sc")
         nc.vector.tensor_copy(d_sc_got[:], d_sc_win[:].indirect(kidx_t[:]))
-        d_sc_dealt = sb([P, H], U8, "d_sc_dealt")
         deal(nc, d_sc_dealt[:], d_sc_got[:])
         for r in range(4):
-            src = 16 * (r // 2) + r % 2
-            nc.scalar.dma_start(d_sc[r:P:32, :].bitcast(I32), d_sc_dealt[src:P:32, :].bitcast(I32))
-        load_tab(0)
-
-        d_got = sb([P, H], U32, "d_got", "tab3")
-        d_q = sb([P, H], U32, "d_q")
-        nc.vector.tensor_copy(d_got[:], d_win[:].indirect(kidx_t[:]))
-        load_tab(1)
+            nc.scalar.dma_start(d_sc[r:P:32, :].bitcast(I32), d_sc_dealt[8 * r : P : 32, :].bitcast(I32))
 
         x_sc = sb([P, S], U8, "x_sc")
         nc.vector.tensor_copy(x_sc[:], x_sc_win[:].indirect(offs_t[:]))
-        load_tab(2)
+        load_tab(0)
+        d_got = sb([P, H], U32, "d_got", "tab2")
+        d_q = sb([P, H], U32, "d_q")
+        nc.vector.tensor_copy(d_got[:], d_win[:].indirect(kidx_t[:]))
+        load_tab(1)
         deal(nc, d_q[:].bitcast(I32), d_got[:].bitcast(I32))
+        load_tab(2)
         load_tab(3)
 
         halves = range(S // HALF)
@@ -142,7 +142,7 @@ def tile_picked_scorebias_sigmoid_po_kernel(
         y_words = [sb([P, HALF], U32, "y_words%d" % h) for h in halves]
         y_sc = sb([P, S], U8, "y_sc")
         out_rows = out_0.rearrange("(p t) j -> p t j", t=PACK)
-        zs, ys, banks = {}, {}, {}
+        zs, ys, banks, floats = {}, {}, {}, {}
 
         def weigh(c):
             j0, n = CHUNKS[c]
@@ -175,16 +175,17 @@ def tile_picked_scorebias_sigmoid_po_kernel(
                 )
             banks[c] = bank
 
-        def store_floats(c):
+        def store_floats(c, copy):
             j0, n = CHUNKS[c]
             y = sb([P, PACK, n], F32, "y%d" % c)
-            nc.scalar.copy(y[:], banks[c][:])
+            copy(y[:], banks[c][:])
+            floats[c] = y
             nc.sync.dma_start(out_rows[:, :, j0 : j0 + n], y[:])
 
-        def round_result(c, copy):
+        def round_result(c, copy, src):
             n = CHUNKS[c][1]
             yb = sb([P, n, PACK], BF16, "yb%d" % c)
-            copy(yb[:], banks[c][:].rearrange("p t j -> p j t"))
+            copy(yb[:], src[:].rearrange("p t j -> p j t"))
             ys[c] = yb
 
         def planes(c):
@@ -199,19 +200,20 @@ def tile_picked_scorebias_sigmoid_po_kernel(
         def store_words(h):
             nc.sync.dma_start(words_of(out_1)[:, h * HALF : (h + 1) * HALF], y_words[h][:].bitcast(I32))
 
-        for t, h in ((0, 0), (1, 0), (0, 1), (1, 1), (2, 0), (3, 0)):
+        for t, h in ((0, 0), (1, 0), (0, 1), (2, 0), (3, 0)):
             sigmoids(t, h)
         deal(nc, w_q[:].bitcast(I32), w_raw[:].bitcast(I32))
         deal(nc, w_sc[:], w_sc_raw[:])
-        sigmoids(2, 1)
+        sigmoids(1, 1)
         weigh(0)
         weigh(1)
         product(0)
         product(1)
+        sigmoids(2, 1)
         sigmoids(3, 1)
         for c in (0, 1):
-            store_floats(c)
-            round_result(c, nc.scalar.copy)
+            store_floats(c, nc.scalar.copy)
+            round_result(c, nc.scalar.copy, banks[c])
         weigh(2)
         weigh(3)
         product(2)
@@ -219,10 +221,10 @@ def tile_picked_scorebias_sigmoid_po_kernel(
         planes(0)
         planes(1)
         store_words(0)
-        round_result(2, nc.scalar.copy)
-        round_result(3, nc.vector.tensor_copy)
-        store_floats(2)
-        store_floats(3)
+        round_result(2, nc.scalar.copy, banks[2])
+        store_floats(2, nc.scalar.copy)
+        store_floats(3, nc.vector.tensor_copy)
+        round_result(3, nc.vector.tensor_copy, floats[3])
         planes(2)
         planes(3)
         store_words(1)

@@ -18,7 +18,7 @@ ALU = mybir.AluOpType
 P = 128
 PACK = 4
 HALF = 256
-CHUNKS = ((0, 128), (128, 128), (256, 128), (384, 128))
+CHUNK = 128
 
 
 def words_of(dram):
@@ -37,194 +37,223 @@ def tile_picked_scorebias_sigmoid_po_kernel(
     nc = tc.nc
     with ExitStack() as ctx:
         keep = ctx.enter_context(tc.tile_pool(name="keep", bufs=1))
+        reuse = ctx.enter_context(tc.tile_pool(name="reuse", bufs=1))
         psum = ctx.enter_context(tc.psum_pool(name="psum", bufs=1))
 
-        def sb(shape, dtype, name, tag=None):
-            return keep.tile(shape, dtype, name=name, tag=tag or name, align_bytes=64)
+        def sb(shape, dtype, name):
+            return keep.tile(shape, dtype, name=name, align_bytes=64)
+
+        def placed(shape, dtype, name, offset):
+            return reuse.tile(shape, dtype, name=name, align_bytes=64, offset=offset)
 
         def load_scale_rows(queue, plane, dram):
             for q in range(4):
                 queue.dma_start(plane[32 * q : 32 * q + 4, :].bitcast(I32), dram[0, 4 * q : 4 * q + 4, :].bitcast(I32))
 
+        tab_bytes = 4 * U
+        at_tab0 = 0
+        at_tab1 = at_tab0 + tab_bytes
+        at_d_win = at_tab1 + tab_bytes
+        at_x_sc = at_d_win + 4 * G
+        at_d_got = at_x_sc + tab_bytes
+        at_x_win = at_d_got + 64 + tab_bytes
+
         kidx_t = keep.tile([P, H // 16], U16, name="kidx_t")
         offs_t = keep.tile([P, S // 16], U16, name="offs_t")
         rel_t = keep.tile([P, S // 16], U16, name="rel_t")
         d_sc_win = sb([P, G], U8, "d_sc_win")
-        x_sc_win = sb([P, T], U8, "x_sc_win", "tab0")
-        d_win = sb([P, G], U32, "d_win", "tab1")
-        x_win = sb([P, T], U32, "x_win", "w_raw")
+        x_sc_win = placed([P, T], U8, "x_sc_win", at_x_sc)
+        d_win = placed([P, G], U32, "d_win", at_d_win)
+        x_win = placed([P, T], U32, "x_win", at_x_win)
 
         tab_rows = tab.rearrange("(p t) u -> p t u", t=PACK)
         tab_t = []
 
-        def load_tab(t):
-            tile = sb([P, U], F32, "tab%d" % t)
+        def load_tab(t, offset):
+            tile = placed([P, U], F32, "tab%d" % t, offset)
             nc.sync.dma_start(tile[:], tab_rows[:, t, :])
             tab_t.append(tile)
 
-        for win in (d_sc_win, x_sc_win):
-            nc.vector.memset(win[:, : G // 2].bitcast(I32), 0)
-            nc.gpsimd.memset(win[:, G // 2 :].bitcast(I32), 0)
+        nc.vector.memset(d_sc_win[:].bitcast(I32), 0)
+        nc.vector.memset(x_sc_win[:, : T // 2].bitcast(I32), 0)
+        nc.gpsimd.memset(x_sc_win[:, T // 2 :].bitcast(I32), 0)
         warm = sb([P, 2], F32, "warm")
-        nc.vector.memset(warm[:, 0:1], 0.0)
+        nc.gpsimd.memset(warm[:, 0:1], 0.0)
         nc.scalar.activation(warm[:, 1:2], warm[:, 0:1], ACT.Sigmoid)
 
+        early = 3 * G // 8
         nc.sync.dma_start(kidx_t[:], kidx)
         nc.sync.dma_start(offs_t[:], offs)
+        nc.sync.dma_start(d_win[:, :early].bitcast(I32), words_of(d_words)[:, :early])
         nc.sync.dma_start(d_sc_win[0:P:8, :].bitcast(I32), d_scales[0].bitcast(I32))
+        nc.sync.dma_start(d_win[:, early:].bitcast(I32), words_of(d_words)[:, early:])
         load_scale_rows(nc.sync, x_sc_win, x_scales)
-        nc.sync.dma_start(d_win[:].bitcast(I32), words_of(d_words))
         nc.sync.dma_start(x_win[:].bitcast(I32), words_of(x_words))
         nc.sync.dma_start(rel_t[:], rel)
-
-        d_sc_got = sb([P, H], U8, "d_sc_got")
-        d_sc_dealt = sb([P, H], U8, "d_sc_dealt", "tab3")
-        d_sc = sb([P, H], U8, "d_sc")
-        nc.vector.tensor_copy(d_sc_got[:], d_sc_win[:].indirect(kidx_t[:]))
-        deal(nc, d_sc_dealt[:], d_sc_got[:])
-        for r in range(4):
-            nc.scalar.dma_start(d_sc[r:P:32, :].bitcast(I32), d_sc_dealt[8 * r : P : 32, :].bitcast(I32))
-
-        x_sc = sb([P, S], U8, "x_sc")
-        nc.vector.tensor_copy(x_sc[:], x_sc_win[:].indirect(offs_t[:]))
-        load_tab(0)
-        d_got = sb([P, H], U32, "d_got", "tab2")
-        d_q = sb([P, H], U32, "d_q")
-        nc.vector.tensor_copy(d_got[:], d_win[:].indirect(kidx_t[:]))
-        load_tab(1)
-        deal(nc, d_q[:].bitcast(I32), d_got[:].bitcast(I32))
-        load_tab(2)
-        load_tab(3)
-
-        halves = range(S // HALF)
-        x_q = []
-        for h in halves:
-            x_q.append(sb([P, HALF], U32, "x_q%d" % h))
-            nc.vector.tensor_copy(x_q[h][:], x_win[:].indirect(offs_t[:, h * 16 : (h + 1) * 16]))
         w_raw = sb([P, N], U32, "w_raw")
         nc.sync.dma_start(w_raw[:].bitcast(I32), words_of(w1_words))
-        w_q = sb([P, N], U32, "w_q")
 
-        score = {}
-        for a in range(2):
-            for h in halves:
-                bank = psum.tile([P, 2, HALF], F32, name="s_bank%d%d" % (h, a), tag="bank%d" % (2 * a + h))
-                for b in range(2):
-                    cols = slice((2 * a + b) * P, (2 * a + b + 1) * P)
-                    nc.tensor.matmul_mx(
-                        out=bank[:, b, :],
-                        lhsT=d_q[:, cols].bitcast(FP8X4),
-                        lhsT_scale=d_sc[:, cols],
-                        rhs=x_q[h][:].bitcast(FP8X4),
-                        rhs_scale=x_sc[:, h * HALF : (h + 1) * HALF],
-                        start=True,
-                        stop=True,
-                    )
-                sc = sb([P, 2, HALF], F32, "score%d%d" % (h, a))
-                nc.scalar.activation(sc[:], bank[:], ACT.Copy, scale=0.0625)
-                score[(h, a)] = sc
-        w_sc_raw = sb([P, N], U8, "w_sc_raw", "x_q0")
-        nc.vector.memset(w_sc_raw[:].bitcast(I32), 0)
+        d_sc_got = placed([P, H], U8, "d_sc_got", at_tab1 - H // 2)
+        d_sc = sb([P, H], U8, "d_sc")
+        nc.vector.tensor_copy(d_sc_got[:], d_sc_win[:].indirect(kidx_t[:]))
+        deal(nc, d_sc[:], d_sc_got[:])
+        for r in range(1, 4):
+            nc.sync.dma_start(d_sc[r:P:32, :].bitcast(I32), d_sc[8 * r : P : 32, :].bitcast(I32))
+        load_tab(0, at_tab0)
+        load_tab(1, at_tab1)
+
+        d_got = placed([P, H], U32, "d_got", at_d_got)
+        d_q = sb([P, H], U32, "d_q")
+        nc.vector.tensor_copy(d_got[:], d_win[:].indirect(kidx_t[:]))
+        w_sc_raw = placed([P, N], U8, "w_sc_raw", at_d_win)
+        nc.gpsimd.memset(w_sc_raw[:].bitcast(I32), 0)
         load_scale_rows(nc.sync, w_sc_raw, w1_scales)
-        w_sc = sb([P, N], U8, "w_sc")
-        gn_t = sb([P, PACK], F32, "gn_t", "x_q1")
+        x_sc = sb([P, S], U8, "x_sc")
+        nc.vector.tensor_copy(x_sc[:], x_sc_win[:].indirect(offs_t[:]))
+        load_tab(2, at_x_sc)
+        deal(nc, d_q[:].bitcast(I32), d_got[:].bitcast(I32))
+        load_tab(3, at_d_got + 64)
+        gn_t = placed([P, PACK], F32, "gn_t", at_d_got)
         nc.sync.dma_start(gn_t[:], gn.rearrange("(p t) o -> p (t o)", t=PACK))
 
-        sig = [sb([P, PACK, HALF], F32, "sig%d" % h) for h in halves]
+        x_q = [sb([P, HALF], U32, "x_q%d" % h) for h in range(2)]
+        for h in range(2):
+            nc.vector.tensor_copy(x_q[h][:], x_win[:].indirect(offs_t[:, h * 16 : (h + 1) * 16]))
+        w_q = placed([P, N], U32, "w_q", at_x_win)
+        w_sc = sb([P, N], U8, "w_sc")
+        deal(nc, w_q[:].bitcast(I32), w_raw[:].bitcast(I32))
+        deal(nc, w_sc[:], w_sc_raw[:])
 
-        def sigmoids(t, h):
-            u = sb([P, HALF], F32, "u%d%d" % (t, h))
-            nc.vector.tensor_tensor(
-                u[:], tab_t[t][:].indirect(rel_t[:, h * 16 : (h + 1) * 16]), score[(h, t // 2)][:, t % 2, :], ALU.add
-            )
-            nc.scalar.activation(sig[h][:, t, :], u[:], ACT.Sigmoid)
+        score = {}
+        u = [sb([P, S], F32, "u%d" % t) for t in range(PACK)]
+        sig = sb([P, 2, PACK, HALF], F32, "sig")
 
-        y_words = [sb([P, HALF], U32, "y_words%d" % h) for h in halves]
-        y_sc = sb([P, S], U8, "y_sc")
-        out_rows = out_0.rearrange("(p t) j -> p t j", t=PACK)
-        zs, ys, banks, floats = {}, {}, {}, {}
-
-        def weigh(c):
-            j0, n = CHUNKS[c]
-            h, lo = divmod(j0, HALF)
-            z = sb([P, n * PACK], BF16, "z%d" % c)
-            nc.vector.tensor_tensor(
-                z[:].rearrange("p (g i t) -> p g t i", i=4, t=PACK),
-                sig[h][:, :, lo : lo + n].rearrange("p t (g i) -> p g t i", i=4),
-                gn_t[:].unsqueeze(1).unsqueeze(3).to_broadcast([P, n // 4, PACK, 4]),
-                ALU.mult,
-            )
-            zs[c] = z
-
-        def product(c):
-            n = CHUNKS[c][1]
-            z_q = sb([P, n], U32, "z_q%d" % c)
-            z_sc = sb([P, n], U8, "z_sc%d" % c)
-            nc.vector.quantize_mx(out=z_q[:].bitcast(FP8X4), scales=z_sc[:], in_=zs[c][:])
-            bank = psum.tile([P, PACK, n], F32, name="y_bank%d" % c, tag="bank%d" % ((4 + c) % 8))
-            for t in range(PACK):
-                wc = slice(t * P, (t + 1) * P)
+        def scores(t, j0, n, bank_no):
+            bank = psum.tile([P, n], F32, name="s_bank%d" % bank_no, tag="bank%d" % bank_no)
+            keys = slice(t * P, (t + 1) * P)
+            for h in range(j0 // HALF, (j0 + n) // HALF):
                 nc.tensor.matmul_mx(
-                    out=bank[:, t, :],
-                    lhsT=w_q[:, wc].bitcast(FP8X4),
-                    lhsT_scale=w_sc[:, wc],
-                    rhs=z_q[:].bitcast(FP8X4),
-                    rhs_scale=z_sc[:],
+                    out=bank[:, h * HALF - j0 : (h + 1) * HALF - j0],
+                    lhsT=d_q[:, keys].bitcast(FP8X4),
+                    lhsT_scale=d_sc[:, keys],
+                    rhs=x_q[h][:].bitcast(FP8X4),
+                    rhs_scale=x_sc[:, h * HALF : (h + 1) * HALF],
                     start=True,
                     stop=True,
                 )
-            banks[c] = bank
+            return bank
 
-        def store_floats(c, copy):
-            j0, n = CHUNKS[c]
-            y = sb([P, PACK, n], F32, "y%d" % c)
-            copy(y[:], banks[c][:])
-            floats[c] = y
-            nc.sync.dma_start(out_rows[:, :, j0 : j0 + n], y[:])
+        def scale_out(t, j0, n, bank, tag):
+            score[t, j0] = keep.tile([P, n], F32, name="score%d_%d" % (t, j0), tag=tag, align_bytes=64)
+            nc.scalar.activation(score[t, j0][:], bank[:], ACT.Copy, scale=0.0625)
+
+        def sigmoids(t, j0, n):
+            cols = slice(j0, j0 + n)
+            nc.vector.tensor_tensor(
+                u[t][:, cols], tab_t[t][:].indirect(rel_t[:, j0 // 16 : (j0 + n) // 16]), score[t, j0][:], ALU.add
+            )
+            nc.scalar.activation(
+                sig[:, j0 // HALF : (j0 + n) // HALF, t, :], u[t][:, cols].rearrange("p (h j) -> p h j", j=HALF), ACT.Sigmoid
+            )
+
+        for t, j0, n, bank_no in ((0, 0, HALF, 0), (0, HALF, HALF, 4), (1, 0, S, 1), (2, 0, S, 2), (3, 0, HALF, 5)):
+            scale_out(t, j0, n, scores(t, j0, n, bank_no), "score%d_%d" % (t, j0))
+        last_bank = scores(3, HALF, HALF, 3)
+        sigmoids(0, 0, HALF)
+        sigmoids(0, HALF, HALF)
+        sigmoids(1, 0, S)
+        scale_out(3, HALF, HALF, last_bank, "u1")
+        idle_bank = psum.tile([P, H], F32, name="idle_bank", tag="bank3")
+        for t in range(2):
+            nc.tensor.matmul_mx(
+                out=idle_bank[:],
+                lhsT=w_q[:, t * P : (t + 1) * P].bitcast(FP8X4),
+                lhsT_scale=w_sc[:, t * P : (t + 1) * P],
+                rhs=d_q[:].bitcast(FP8X4),
+                rhs_scale=d_sc[:],
+                start=True,
+                stop=True,
+            )
+        sigmoids(2, 0, S)
+        sigmoids(3, 0, HALF)
+        sigmoids(3, HALF, HALF)
+
+        y_words = [sb([P, HALF], U32, "y_words%d" % h) for h in range(2)]
+        y_sc = sb([P, S], U8, "y_sc")
+        out_rows = out_0.rearrange("(p t) j -> p t j", t=PACK)
+        n = CHUNK
+        chunks = range(S // n)
+        z = [sb([P, n * PACK], BF16, "z%d" % c) for c in chunks]
+        y = [sb([P, PACK, n], F32, "y%d" % c) for c in chunks]
+        y_bf = [sb([P, n, PACK], BF16, "y_bf%d" % c) for c in chunks]
+        banks = {}
+
+        def weigh(c, lo, width):
+            h, j0 = divmod(c * n + lo, HALF)
+            nc.vector.tensor_tensor(
+                z[c][:, lo * PACK : (lo + width) * PACK].rearrange("p (g i t) -> p g t i", i=4, t=PACK),
+                sig[:, h, :, j0 : j0 + width].rearrange("p t (g i) -> p g t i", i=4),
+                gn_t[:].unsqueeze(1).unsqueeze(3).to_broadcast([P, width // 4, PACK, 4]),
+                ALU.mult,
+            )
+
+        def product(c, bank_nos):
+            z_q = sb([P, n], U32, "z_q%d" % c)
+            z_sc = sb([P, n], U8, "z_sc%d" % c)
+            nc.vector.quantize_mx(out=z_q[:].bitcast(FP8X4), scales=z_sc[:], in_=z[c][:])
+            per_bank = PACK // len(bank_nos)
+            banks[c] = []
+            for b, bank_no in enumerate(bank_nos):
+                bank = psum.tile([P, per_bank, n], F32, name="y_bank%d_%d" % (c, b), tag="bank%d" % bank_no)
+                for i in range(per_bank):
+                    wc = slice((b * per_bank + i) * P, (b * per_bank + i + 1) * P)
+                    nc.tensor.matmul_mx(
+                        out=bank[:, i, :],
+                        lhsT=w_q[:, wc].bitcast(FP8X4),
+                        lhsT_scale=w_sc[:, wc],
+                        rhs=z_q[:].bitcast(FP8X4),
+                        rhs_scale=z_sc[:],
+                        start=True,
+                        stop=True,
+                    )
+                banks[c].append(bank)
+
+        def store_floats(c):
+            nc.sync.dma_start(out_rows[:, :, c * n : (c + 1) * n], y[c][:])
 
         def round_result(c, copy, src):
-            n = CHUNKS[c][1]
-            yb = sb([P, n, PACK], BF16, "yb%d" % c)
-            copy(yb[:], src[:].rearrange("p t j -> p j t"))
-            ys[c] = yb
+            copy(y_bf[c][:], src[:].rearrange("p t j -> p j t"))
 
         def planes(c):
-            j0, n = CHUNKS[c]
-            h, lo = divmod(j0, HALF)
+            h, lo = divmod(c * n, HALF)
             nc.vector.quantize_mx(
                 out=y_words[h][:, lo : lo + n].bitcast(FP8X4),
-                scales=y_sc[:, j0 : j0 + n],
-                in_=ys[c][:].rearrange("p j t -> p (j t)"),
+                scales=y_sc[:, c * n : (c + 1) * n],
+                in_=y_bf[c][:].rearrange("p j t -> p (j t)"),
             )
 
         def store_words(h):
             nc.sync.dma_start(words_of(out_1)[:, h * HALF : (h + 1) * HALF], y_words[h][:].bitcast(I32))
 
-        for t, h in ((0, 0), (1, 0), (0, 1), (2, 0), (3, 0)):
-            sigmoids(t, h)
-        deal(nc, w_q[:].bitcast(I32), w_raw[:].bitcast(I32))
-        deal(nc, w_sc[:], w_sc_raw[:])
-        sigmoids(1, 1)
-        weigh(0)
-        weigh(1)
-        product(0)
-        product(1)
-        sigmoids(2, 1)
-        sigmoids(3, 1)
-        for c in (0, 1):
-            store_floats(c, nc.scalar.copy)
-            round_result(c, nc.scalar.copy, banks[c])
-        weigh(2)
-        weigh(3)
-        product(2)
-        product(3)
+        weigh(0, 0, n)
+        for c, bank_nos in enumerate(((5,), (6,), (7,))):
+            weigh(c + 1, 0, n // 2)
+            product(c, bank_nos)
+            weigh(c + 1, n // 2, n // 2)
+        product(3, (0, 4))
+        for c in range(3):
+            nc.scalar.copy(y[c][:], banks[c][0][:])
+            store_floats(c)
+        nc.scalar.copy(y[3][:, :2, :], banks[3][0][:])
+        round_result(2, nc.scalar.copy, banks[2][0])
+        round_result(0, nc.vector.tensor_copy, y[0])
+        round_result(1, nc.vector.tensor_copy, y[1])
         planes(0)
+        nc.vector.tensor_copy(y[3][:, 2:, :], banks[3][1][:])
+        store_floats(3)
         planes(1)
         store_words(0)
-        round_result(2, nc.scalar.copy, banks[2])
-        store_floats(2, nc.scalar.copy)
-        store_floats(3, nc.vector.tensor_copy)
-        round_result(3, nc.vector.tensor_copy, floats[3])
+        round_result(3, nc.vector.tensor_copy, y[3])
         planes(2)
         planes(3)
         store_words(1)

@@ -55,8 +55,8 @@ def tile_picked_scorebias_sigmoid_po_kernel(
         at_tab1 = at_tab0 + tab_bytes
         at_d_win = at_tab1 + tab_bytes
         at_x_sc = at_d_win + 4 * G
-        at_d_got = at_x_sc + tab_bytes
-        at_x_win = at_d_got + 64 + tab_bytes
+        at_w_q = at_x_sc + tab_bytes
+        at_d_got = at_w_q + 4 * N - 64
 
         kidx_t = keep.tile([P, H // 16], U16, name="kidx_t")
         offs_t = keep.tile([P, S // 16], U16, name="offs_t")
@@ -64,7 +64,7 @@ def tile_picked_scorebias_sigmoid_po_kernel(
         d_sc_win = sb([P, G], U8, "d_sc_win")
         x_sc_win = placed([P, T], U8, "x_sc_win", at_x_sc)
         d_win = placed([P, G], U32, "d_win", at_d_win)
-        x_win = placed([P, T], U32, "x_win", at_x_win)
+        x_win = sb([P, T], U32, "x_win")
 
         tab_rows = tab.rearrange("(p t) u -> p t u", t=PACK)
         tab_t = []
@@ -81,7 +81,7 @@ def tile_picked_scorebias_sigmoid_po_kernel(
         nc.gpsimd.memset(warm[:, 0:1], 0.0)
         nc.scalar.activation(warm[:, 1:2], warm[:, 0:1], ACT.Sigmoid)
 
-        early = 3 * G // 8
+        early = G // 4
         nc.sync.dma_start(kidx_t[:], kidx)
         nc.sync.dma_start(offs_t[:], offs)
         nc.sync.dma_start(d_win[:, :early].bitcast(I32), words_of(d_words)[:, :early])
@@ -112,14 +112,14 @@ def tile_picked_scorebias_sigmoid_po_kernel(
         nc.vector.tensor_copy(x_sc[:], x_sc_win[:].indirect(offs_t[:]))
         load_tab(2, at_x_sc)
         deal(nc, d_q[:].bitcast(I32), d_got[:].bitcast(I32))
-        load_tab(3, at_d_got + 64)
-        gn_t = placed([P, PACK], F32, "gn_t", at_d_got)
+        load_tab(3, at_d_got + 128)
+        gn_t = placed([P, PACK], F32, "gn_t", at_d_got + 64)
         nc.sync.dma_start(gn_t[:], gn.rearrange("(p t) o -> p (t o)", t=PACK))
 
         x_q = [sb([P, HALF], U32, "x_q%d" % h) for h in range(2)]
         for h in range(2):
             nc.vector.tensor_copy(x_q[h][:], x_win[:].indirect(offs_t[:, h * 16 : (h + 1) * 16]))
-        w_q = placed([P, N], U32, "w_q", at_x_win)
+        w_q = placed([P, N], U32, "w_q", at_w_q)
         w_sc = sb([P, N], U8, "w_sc")
         deal(nc, w_q[:].bitcast(I32), w_raw[:].bitcast(I32))
         deal(nc, w_sc[:], w_sc_raw[:])
@@ -221,8 +221,11 @@ def tile_picked_scorebias_sigmoid_po_kernel(
         def store_floats(c):
             nc.sync.dma_start(out_rows[:, :, c * n : (c + 1) * n], y[c][:])
 
-        def round_result(c, copy, src):
-            copy(y_bf[c][:], src[:].rearrange("p t j -> p j t"))
+        def interleave(copy, dst, src):
+            copy(dst.rearrange("p (g i) t -> p g t i", i=4), src.rearrange("p t (g i) -> p g t i", i=4))
+
+        def round_result(c):
+            interleave(nc.vector.tensor_copy, y_bf[c][:], y[c][:])
 
         def planes(c):
             h, lo = divmod(c * n, HALF)
@@ -235,25 +238,30 @@ def tile_picked_scorebias_sigmoid_po_kernel(
         def store_words(h):
             nc.sync.dma_start(words_of(out_1)[:, h * HALF : (h + 1) * HALF], y_words[h][:].bitcast(I32))
 
+        z_rows = sb([P, PACK, n], BF16, "z_rows")
+        for t in range(PACK):
+            nc.scalar.activation(z_rows[:, t, :], sig[:, 1, t, HALF - n :], ACT.Copy, scale=gn_t[:, t : t + 1])
+        interleave(nc.scalar.copy, z[3][:].rearrange("p (j t) -> p j t", t=PACK), z_rows[:])
         weigh(0, 0, n)
-        for c, bank_nos in enumerate(((5,), (6,), (7,))):
+        for c, bank_nos in enumerate(((5,), (6,))):
             weigh(c + 1, 0, n // 2)
             product(c, bank_nos)
             weigh(c + 1, n // 2, n // 2)
+        product(2, (7,))
         product(3, (0, 4))
         for c in range(3):
             nc.scalar.copy(y[c][:], banks[c][0][:])
             store_floats(c)
-        nc.scalar.copy(y[3][:, :2, :], banks[3][0][:])
-        round_result(2, nc.scalar.copy, banks[2][0])
-        round_result(0, nc.vector.tensor_copy, y[0])
-        round_result(1, nc.vector.tensor_copy, y[1])
+        nc.scalar.copy(y_bf[2][:], banks[2][0][:].rearrange("p t j -> p j t"))
+        round_result(0)
         planes(0)
+        nc.vector.tensor_copy(y[3][:, :2, :], banks[3][0][:])
         nc.vector.tensor_copy(y[3][:, 2:, :], banks[3][1][:])
         store_floats(3)
+        round_result(1)
+        round_result(3)
         planes(1)
         store_words(0)
-        round_result(3, nc.vector.tensor_copy, y[3])
         planes(2)
         planes(3)
         store_words(1)

@@ -184,7 +184,8 @@ def tile_picked_scorebias_sigmoid_po_kernel(
         n = CHUNK
         chunks = range(S // n)
         z = [sb([P, n * PACK], BF16, "z%d" % c) for c in chunks]
-        y = [sb([P, PACK, n], F32, "y%d" % c) for c in chunks]
+        y_late = sb([P, PACK, HALF], F32, "y_late")
+        y = [sb([P, PACK, n], F32, "y0")[:], sb([P, PACK, n], F32, "y1")[:], y_late[:, :, :n], y_late[:, :, n:]]
         y_bf = [sb([P, n, PACK], BF16, "y_bf%d" % c) for c in chunks]
         banks = {}
 
@@ -218,14 +219,12 @@ def tile_picked_scorebias_sigmoid_po_kernel(
                     )
                 banks[c].append(bank)
 
-        def store_floats(c):
-            nc.sync.dma_start(out_rows[:, :, c * n : (c + 1) * n], y[c][:])
 
         def interleave(copy, dst, src):
             copy(dst.rearrange("p (g i) t -> p g t i", i=4), src.rearrange("p t (g i) -> p g t i", i=4))
 
         def round_result(c):
-            interleave(nc.vector.tensor_copy, y_bf[c][:], y[c][:])
+            interleave(nc.vector.tensor_copy, y_bf[c][:], y[c])
 
         def planes(c):
             h, lo = divmod(c * n, HALF)
@@ -243,21 +242,24 @@ def tile_picked_scorebias_sigmoid_po_kernel(
             nc.scalar.activation(z_rows[:, t, :], sig[:, 1, t, HALF - n :], ACT.Copy, scale=gn_t[:, t : t + 1])
         interleave(nc.scalar.copy, z[3][:].rearrange("p (j t) -> p j t", t=PACK), z_rows[:])
         weigh(0, 0, n)
-        for c, bank_nos in enumerate(((5,), (6,))):
+        for c, bank_nos in enumerate(((1, 2), (6,))):
             weigh(c + 1, 0, n // 2)
             product(c, bank_nos)
             weigh(c + 1, n // 2, n // 2)
         product(2, (7,))
         product(3, (0, 4))
-        for c in range(3):
-            nc.scalar.copy(y[c][:], banks[c][0][:])
-            store_floats(c)
+        for b in range(2):
+            nc.scalar.copy(y[0][:, 2 * b : 2 * b + 2, :], banks[0][b][:])
+            nc.sync.dma_start(out_rows[:, 2 * b : 2 * b + 2, :n], y[0][:, 2 * b : 2 * b + 2, :])
+        nc.scalar.copy(y[1], banks[1][0][:])
+        nc.sync.dma_start(out_rows[:, :, n:HALF], y[1])
+        nc.scalar.copy(y[2], banks[2][0][:])
         nc.scalar.copy(y_bf[2][:], banks[2][0][:].rearrange("p t j -> p j t"))
         round_result(0)
         planes(0)
         nc.vector.tensor_copy(y[3][:, :2, :], banks[3][0][:])
         nc.vector.tensor_copy(y[3][:, 2:, :], banks[3][1][:])
-        store_floats(3)
+        nc.sync.dma_start(out_rows[:, :, HALF:], y_late[:])
         round_result(1)
         round_result(3)
         planes(1)

@@ -52,8 +52,8 @@ def tile_picked_scorebias_sigmoid_po_kernel(
 
         tab_bytes = 4 * U
         at_tab0 = 0
-        at_tab1 = at_tab0 + tab_bytes
-        at_d_win = at_tab1 + tab_bytes
+        at_w_sc = at_tab0 + tab_bytes
+        at_d_win = at_w_sc + N
         at_x_sc = at_d_win + 4 * G
         at_w_q = at_x_sc + tab_bytes
         at_d_got = at_w_q + 4 * N - 64
@@ -93,21 +93,21 @@ def tile_picked_scorebias_sigmoid_po_kernel(
         w_raw = sb([P, N], U32, "w_raw")
         nc.sync.dma_start(w_raw[:].bitcast(I32), words_of(w1_words))
 
-        d_sc_got = placed([P, H], U8, "d_sc_got", at_tab1 - H // 2)
+        d_sc_got = placed([P, H], U8, "d_sc_got", at_w_sc - H // 2)
         d_sc = sb([P, H], U8, "d_sc")
         nc.vector.tensor_copy(d_sc_got[:], d_sc_win[:].indirect(kidx_t[:]))
         deal(nc, d_sc[:], d_sc_got[:])
         for r in range(1, 4):
             nc.sync.dma_start(d_sc[r:P:32, :].bitcast(I32), d_sc[8 * r : P : 32, :].bitcast(I32))
         load_tab(0, at_tab0)
-        load_tab(1, at_tab1)
+        w_sc_raw = placed([P, N], U8, "w_sc_raw", at_w_sc)
+        nc.gpsimd.memset(w_sc_raw[:].bitcast(I32), 0)
+        load_scale_rows(nc.sync, w_sc_raw, w1_scales)
 
         d_got = placed([P, H], U32, "d_got", at_d_got)
         d_q = sb([P, H], U32, "d_q")
         nc.vector.tensor_copy(d_got[:], d_win[:].indirect(kidx_t[:]))
-        w_sc_raw = placed([P, N], U8, "w_sc_raw", at_d_win)
-        nc.gpsimd.memset(w_sc_raw[:].bitcast(I32), 0)
-        load_scale_rows(nc.sync, w_sc_raw, w1_scales)
+        load_tab(1, at_d_win)
         x_sc = sb([P, S], U8, "x_sc")
         nc.vector.tensor_copy(x_sc[:], x_sc_win[:].indirect(offs_t[:]))
         load_tab(2, at_x_sc)

@@ -17,18 +17,33 @@ ALU = mybir.AluOpType
 
 P = 128
 PACK = 4
+GROUP = 16
 HALF = 256
 CHUNK = 128
+PAIR = 2
+LINE = 4
+BANKS = 8
+ALIGN = 64
 
 
 def words_of(dram):
     return dram[0].rearrange("p n r -> p (n r)").bitcast(I32)
 
 
-def deal(nc, dst, src):
+def entries(list_tile, first, count):
+    return list_tile[:, first // GROUP : (first + count) // GROUP]
+
+
+def deal(nc, dst, src, first):
+    runs = slice(first // (PACK * LINE), (first + src.shape[1]) // (PACK * LINE))
     nc.vector.tensor_copy(
-        dst.rearrange("p (t g i) -> p g t i", t=PACK, i=4), src.rearrange("p (g i t) -> p g t i", t=PACK, i=4)
+        dst.rearrange("p (t g i) -> p g t i", t=PACK, i=LINE)[:, runs],
+        src.rearrange("p (g i t) -> p g t i", t=PACK, i=LINE),
     )
+
+
+def interleave(copy, dst, src):
+    copy(dst.rearrange("p (g i) t -> p g t i", i=LINE), src.rearrange("p t (g i) -> p g t i", i=LINE))
 
 
 def tile_picked_scorebias_sigmoid_po_kernel(
@@ -41,38 +56,57 @@ def tile_picked_scorebias_sigmoid_po_kernel(
         psum = ctx.enter_context(tc.psum_pool(name="psum", bufs=1))
 
         def sb(shape, dtype, name):
-            return keep.tile(shape, dtype, name=name, align_bytes=64)
+            return keep.tile(shape, dtype, name=name, align_bytes=ALIGN)
 
         def placed(shape, dtype, name, offset):
-            return reuse.tile(shape, dtype, name=name, align_bytes=64, offset=offset)
+            return reuse.tile(shape, dtype, name=name, align_bytes=ALIGN, offset=offset)
 
-        def load_scale_rows(queue, plane, dram):
-            for q in range(4):
-                queue.dma_start(plane[32 * q : 32 * q + 4, :].bitcast(I32), dram[0, 4 * q : 4 * q + 4, :].bitcast(I32))
+        def bank_tile(shape, number, name):
+            return psum.tile(shape, F32, name=name, tag="bank%d" % number)
+
+        def load_spread(plane, dram):
+            nc.sync.dma_start(plane[0:P:8, :].bitcast(I32), dram[0].bitcast(I32))
+
+        def close_up(plane):
+            for r in range(1, 4):
+                nc.sync.dma_start(plane[r:P:32, :].bitcast(I32), plane[8 * r : P : 32, :].bitcast(I32))
+
+        def matmul(out, lhsT, lhsT_scale, rhs, rhs_scale):
+            nc.tensor.matmul_mx(
+                out=out,
+                lhsT=lhsT.bitcast(FP8X4),
+                lhsT_scale=lhsT_scale,
+                rhs=rhs.bitcast(FP8X4),
+                rhs_scale=rhs_scale,
+                start=True,
+                stop=True,
+            )
 
         tab_bytes = 4 * U
-        at_tab0 = 0
-        at_w_sc = at_tab0 + tab_bytes
-        at_d_win = at_w_sc + N
-        at_x_sc = at_d_win + 4 * G
-        at_w_q = at_x_sc + tab_bytes
-        at_d_got = at_w_q + 4 * N - 64
+        at_w_raw = 0
+        at_w_sc_raw = at_w_raw + 4 * N
+        at_tab0 = at_w_sc_raw + N
+        at_d_win = at_tab0 + tab_bytes
+        at_x_sc_win = at_d_win + 4 * G
+        at_w_q = at_x_sc_win + tab_bytes
+        at_gn = at_w_q + 4 * N
+        at_tab3 = at_gn + ALIGN
 
-        kidx_t = keep.tile([P, H // 16], U16, name="kidx_t")
-        offs_t = keep.tile([P, S // 16], U16, name="offs_t")
-        rel_t = keep.tile([P, S // 16], U16, name="rel_t")
+        kidx_t = keep.tile([P, H // GROUP], U16, name="kidx_t")
+        offs_t = keep.tile([P, S // GROUP], U16, name="offs_t")
+        rel_t = keep.tile([P, S // GROUP], U16, name="rel_t")
         d_sc_win = sb([P, G], U8, "d_sc_win")
-        x_sc_win = placed([P, T], U8, "x_sc_win", at_x_sc)
+        x_sc_win = placed([P, T], U8, "x_sc_win", at_x_sc_win)
         d_win = placed([P, G], U32, "d_win", at_d_win)
         x_win = sb([P, T], U32, "x_win")
 
         tab_rows = tab.rearrange("(p t) u -> p t u", t=PACK)
         tab_t = []
 
-        def load_tab(t, offset):
-            tile = placed([P, U], F32, "tab%d" % t, offset)
-            nc.sync.dma_start(tile[:], tab_rows[:, t, :])
-            tab_t.append(tile)
+        def load_tab(offset):
+            t = len(tab_t)
+            tab_t.append(placed([P, U], F32, "tab%d" % t, offset))
+            nc.sync.dma_start(tab_t[t][:], tab_rows[:, t, :])
 
         nc.vector.memset(d_sc_win[:].bitcast(I32), 0)
         nc.vector.memset(x_sc_win[:, : T // 2].bitcast(I32), 0)
@@ -85,188 +119,166 @@ def tile_picked_scorebias_sigmoid_po_kernel(
         nc.sync.dma_start(kidx_t[:], kidx)
         nc.sync.dma_start(offs_t[:], offs)
         nc.sync.dma_start(d_win[:, :early].bitcast(I32), words_of(d_words)[:, :early])
-        nc.sync.dma_start(d_sc_win[0:P:8, :].bitcast(I32), d_scales[0].bitcast(I32))
+        load_spread(d_sc_win, d_scales)
         nc.sync.dma_start(d_win[:, early:].bitcast(I32), words_of(d_words)[:, early:])
-        load_scale_rows(nc.sync, x_sc_win, x_scales)
+        for q in range(4):
+            nc.sync.dma_start(x_sc_win[32 * q : 32 * q + 4, :].bitcast(I32), x_scales[0, 4 * q : 4 * q + 4, :].bitcast(I32))
         nc.sync.dma_start(x_win[:].bitcast(I32), words_of(x_words))
         nc.sync.dma_start(rel_t[:], rel)
-        w_raw = sb([P, N], U32, "w_raw")
-        nc.sync.dma_start(w_raw[:].bitcast(I32), words_of(w1_words))
 
-        d_sc_got = placed([P, H], U8, "d_sc_got", at_w_sc - H // 2)
+        def pick_keys(dealt, halves, window, move_as):
+            for h, got in enumerate(halves):
+                nc.vector.tensor_copy(got, window[:].indirect(entries(kidx_t, h * HALF, HALF)))
+            for h, got in enumerate(halves):
+                deal(nc, dealt[:].bitcast(move_as), got.bitcast(move_as), h * HALF)
+
         d_sc = sb([P, H], U8, "d_sc")
-        nc.vector.tensor_copy(d_sc_got[:], d_sc_win[:].indirect(kidx_t[:]))
-        deal(nc, d_sc[:], d_sc_got[:])
-        for r in range(1, 4):
-            nc.sync.dma_start(d_sc[r:P:32, :].bitcast(I32), d_sc[8 * r : P : 32, :].bitcast(I32))
-        load_tab(0, at_tab0)
-        w_sc_raw = placed([P, N], U8, "w_sc_raw", at_w_sc)
+        d_sc_hold = placed([P, N + 2 * ALIGN], U8, "d_sc_got1", at_w_sc_raw - ALIGN)
+        pick_keys(d_sc, (sb([P, HALF], U8, "d_sc_got0")[:], d_sc_hold[:, :HALF]), d_sc_win, U8)
+        close_up(d_sc)
+        w_raw = placed([P, N], U32, "w_raw", at_w_raw)
+        nc.sync.dma_start(w_raw[:].bitcast(I32), words_of(w1_words))
+        load_tab(at_tab0)
+        w_sc_raw = placed([P, N], U8, "w_sc_raw", at_w_sc_raw)
         nc.gpsimd.memset(w_sc_raw[:].bitcast(I32), 0)
-        load_scale_rows(nc.sync, w_sc_raw, w1_scales)
+        load_spread(w_sc_raw, w1_scales)
 
-        d_got = placed([P, H], U32, "d_got", at_d_got)
         d_q = sb([P, H], U32, "d_q")
-        nc.vector.tensor_copy(d_got[:], d_win[:].indirect(kidx_t[:]))
-        load_tab(1, at_d_win)
+        d_hold = placed([P, HALF], U32, "d_got1", at_gn - ALIGN)
+        pick_keys(d_q, (sb([P, HALF], U32, "d_got0")[:], d_hold[:]), d_win, I32)
+        load_tab(at_d_win)
         x_sc = sb([P, S], U8, "x_sc")
         nc.vector.tensor_copy(x_sc[:], x_sc_win[:].indirect(offs_t[:]))
-        load_tab(2, at_x_sc)
-        deal(nc, d_q[:].bitcast(I32), d_got[:].bitcast(I32))
-        load_tab(3, at_d_got + 128)
-        gn_t = placed([P, PACK], F32, "gn_t", at_d_got + 64)
+        load_tab(at_x_sc_win)
+        load_tab(at_tab3)
+        gn_t = placed([P, PACK], F32, "gn_t", at_gn)
         nc.sync.dma_start(gn_t[:], gn.rearrange("(p t) o -> p (t o)", t=PACK))
 
         x_q = [sb([P, HALF], U32, "x_q%d" % h) for h in range(2)]
         for h in range(2):
-            nc.vector.tensor_copy(x_q[h][:], x_win[:].indirect(offs_t[:, h * 16 : (h + 1) * 16]))
+            nc.vector.tensor_copy(x_q[h][:], x_win[:].indirect(entries(offs_t, h * HALF, HALF)))
         w_q = placed([P, N], U32, "w_q", at_w_q)
         w_sc = sb([P, N], U8, "w_sc")
-        deal(nc, w_q[:].bitcast(I32), w_raw[:].bitcast(I32))
-        deal(nc, w_sc[:], w_sc_raw[:])
+        deal(nc, w_q[:].bitcast(I32), w_raw[:].bitcast(I32), 0)
+        deal(nc, w_sc[:], w_sc_raw[:], 0)
+        close_up(w_sc)
 
-        score = {}
-        u = [sb([P, S], F32, "u%d" % t) for t in range(PACK)]
+        score = [sb([P, S], F32, "score%d" % t) for t in range(PACK)]
+        biased = [placed([P, S], F32, "biased0", at_tab0 - 4 * S)]
+        biased.extend(sb([P, S], F32, "biased%d" % t) for t in range(1, PACK))
         sig = sb([P, 2, PACK, HALF], F32, "sig")
+        z_rows = sb([P, PACK, CHUNK], BF16, "z_rows")
 
-        def scores(t, j0, n, bank_no):
-            bank = psum.tile([P, n], F32, name="s_bank%d" % bank_no, tag="bank%d" % bank_no)
+        def scores(t, first, count, bank_number):
+            bank = bank_tile([P, count], bank_number, "score_bank%d" % bank_number)
             keys = slice(t * P, (t + 1) * P)
-            for h in range(j0 // HALF, (j0 + n) // HALF):
-                nc.tensor.matmul_mx(
-                    out=bank[:, h * HALF - j0 : (h + 1) * HALF - j0],
-                    lhsT=d_q[:, keys].bitcast(FP8X4),
-                    lhsT_scale=d_sc[:, keys],
-                    rhs=x_q[h][:].bitcast(FP8X4),
-                    rhs_scale=x_sc[:, h * HALF : (h + 1) * HALF],
-                    start=True,
-                    stop=True,
-                )
-            return bank
+            for lo in range(0, count, HALF):
+                cols = slice(first + lo, first + lo + HALF)
+                matmul(bank[:, lo : lo + HALF], d_q[:, keys], d_sc[:, keys], x_q[cols.start // HALF][:], x_sc[:, cols])
+            nc.scalar.activation(score[t][:, first : first + count], bank[:], ACT.Copy, scale=0.0625)
 
-        def scale_out(t, j0, n, bank, tag):
-            score[t, j0] = keep.tile([P, n], F32, name="score%d_%d" % (t, j0), tag=tag, align_bytes=64)
-            nc.scalar.activation(score[t, j0][:], bank[:], ACT.Copy, scale=0.0625)
-
-        def sigmoids(t, j0, n):
-            cols = slice(j0, j0 + n)
+        def add_biases(t, first, count):
+            cols = slice(first, first + count)
             nc.vector.tensor_tensor(
-                u[t][:, cols], tab_t[t][:].indirect(rel_t[:, j0 // 16 : (j0 + n) // 16]), score[t, j0][:], ALU.add
-            )
-            nc.scalar.activation(
-                sig[:, j0 // HALF : (j0 + n) // HALF, t, :], u[t][:, cols].rearrange("p (h j) -> p h j", j=HALF), ACT.Sigmoid
+                biased[t][:, cols], tab_t[t][:].indirect(entries(rel_t, first, count)), score[t][:, cols], ALU.add
             )
 
-        for t, j0, n, bank_no in ((0, 0, HALF, 0), (0, HALF, HALF, 4), (1, 0, S, 1), (2, 0, S, 2), (3, 0, HALF, 5)):
-            scale_out(t, j0, n, scores(t, j0, n, bank_no), "score%d_%d" % (t, j0))
-        last_bank = scores(3, HALF, HALF, 3)
-        sigmoids(0, 0, HALF)
-        sigmoids(0, HALF, HALF)
-        sigmoids(1, 0, S)
-        scale_out(3, HALF, HALF, last_bank, "u1")
-        idle_bank = psum.tile([P, H], F32, name="idle_bank", tag="bank3")
-        for t in range(2):
-            nc.tensor.matmul_mx(
-                out=idle_bank[:],
-                lhsT=w_q[:, t * P : (t + 1) * P].bitcast(FP8X4),
-                lhsT_scale=w_sc[:, t * P : (t + 1) * P],
-                rhs=d_q[:].bitcast(FP8X4),
-                rhs_scale=d_sc[:],
-                start=True,
-                stop=True,
-            )
-        sigmoids(2, 0, S)
+        def sigmoids(t, first, count):
+            h, lo = divmod(first, HALF)
+            nc.scalar.activation(sig[:, h, t, lo : lo + count], biased[t][:, first : first + count], ACT.Sigmoid)
+
+        def weigh_on_scalar(t):
+            nc.scalar.activation(z_rows[:, t, :], sig[:, 1, t, :CHUNK], ACT.Copy, scale=gn_t[:, t : t + 1])
+
+        scores(0, 0, HALF, 0)
+        scores(0, HALF, HALF, PACK)
+        for t in range(1, PACK):
+            scores(t, 0, S, t)
+        for first in (0, HALF):
+            add_biases(0, first, HALF)
+            sigmoids(0, first, HALF)
+        weigh_on_scalar(0)
+        for t in (1, 2):
+            add_biases(t, 0, S)
+            sigmoids(t, HALF, HALF)
+            sigmoids(t, 0, HALF)
+            weigh_on_scalar(t)
+        add_biases(3, 0, HALF)
         sigmoids(3, 0, HALF)
-        sigmoids(3, HALF, HALF)
+        add_biases(3, HALF, HALF)
+        sigmoids(3, HALF, CHUNK)
+        sigmoids(3, HALF + CHUNK, CHUNK)
+        weigh_on_scalar(3)
 
+        chunks = range(S // CHUNK)
+        pairs = [slice(lo, lo + PAIR) for lo in range(0, PACK, PAIR)]
+        z = [sb([P, CHUNK, PACK], BF16, "z%d" % c) for c in chunks]
+        y_late = sb([P, PACK, HALF], F32, "y_late")
+        y = [sb([P, PACK, CHUNK], F32, "y0")[:], sb([P, PACK, CHUNK], F32, "y1")[:], y_late[:, :, :CHUNK], y_late[:, :, CHUNK:]]
+        y_bf = [sb([P, CHUNK, PACK], BF16, "y_bf%d" % c) for c in chunks]
         y_words = [sb([P, HALF], U32, "y_words%d" % h) for h in range(2)]
         y_sc = sb([P, S], U8, "y_sc")
         out_rows = out_0.rearrange("(p t) j -> p t j", t=PACK)
-        n = CHUNK
-        chunks = range(S // n)
-        z = [sb([P, n * PACK], BF16, "z%d" % c) for c in chunks]
-        y_late = sb([P, PACK, HALF], F32, "y_late")
-        y = [sb([P, PACK, n], F32, "y0")[:], sb([P, PACK, n], F32, "y1")[:], y_late[:, :, :n], y_late[:, :, n:]]
-        y_bf = [sb([P, n, PACK], BF16, "y_bf%d" % c) for c in chunks]
         banks = {}
 
-        def weigh(c, lo, width):
-            h, j0 = divmod(c * n + lo, HALF)
+        def weigh(c, lo, count):
+            h, first = divmod(c * CHUNK + lo, HALF)
             nc.vector.tensor_tensor(
-                z[c][:, lo * PACK : (lo + width) * PACK].rearrange("p (g i t) -> p g t i", i=4, t=PACK),
-                sig[:, h, :, j0 : j0 + width].rearrange("p t (g i) -> p g t i", i=4),
-                gn_t[:].unsqueeze(1).unsqueeze(3).to_broadcast([P, width // 4, PACK, 4]),
+                z[c][:, lo : lo + count, :].rearrange("p (g i) t -> p g t i", i=LINE),
+                sig[:, h, :, first : first + count].rearrange("p t (g i) -> p g t i", i=LINE),
+                gn_t[:].unsqueeze(1).unsqueeze(3).to_broadcast([P, count // LINE, PACK, LINE]),
                 ALU.mult,
             )
 
-        def product(c, bank_nos):
-            z_q = sb([P, n], U32, "z_q%d" % c)
-            z_sc = sb([P, n], U8, "z_sc%d" % c)
-            nc.vector.quantize_mx(out=z_q[:].bitcast(FP8X4), scales=z_sc[:], in_=z[c][:])
-            per_bank = PACK // len(bank_nos)
-            banks[c] = []
-            for b, bank_no in enumerate(bank_nos):
-                bank = psum.tile([P, per_bank, n], F32, name="y_bank%d_%d" % (c, b), tag="bank%d" % bank_no)
-                for i in range(per_bank):
-                    wc = slice((b * per_bank + i) * P, (b * per_bank + i + 1) * P)
-                    nc.tensor.matmul_mx(
-                        out=bank[:, i, :],
-                        lhsT=w_q[:, wc].bitcast(FP8X4),
-                        lhsT_scale=w_sc[:, wc],
-                        rhs=z_q[:].bitcast(FP8X4),
-                        rhs_scale=z_sc[:],
-                        start=True,
-                        stop=True,
-                    )
-                banks[c].append(bank)
-
-
-        def interleave(copy, dst, src):
-            copy(dst.rearrange("p (g i) t -> p g t i", i=4), src.rearrange("p t (g i) -> p g t i", i=4))
-
-        def round_result(c):
-            interleave(nc.vector.tensor_copy, y_bf[c][:], y[c])
+        def product(c):
+            z_q = sb([P, CHUNK], U32, "z_q%d" % c)
+            z_sc = sb([P, CHUNK], U8, "z_sc%d" % c)
+            nc.vector.quantize_mx(out=z_q[:].bitcast(FP8X4), scales=z_sc[:], in_=z[c][:].rearrange("p j t -> p (j t)"))
+            for b, pair in enumerate(pairs):
+                banks[c, b] = bank_tile([P, PAIR, CHUNK], (PACK + 1 + len(pairs) * c + b) % BANKS, "y_bank%d_%d" % (c, b))
+                for t in range(pair.start, pair.stop):
+                    rows = slice(t * P, (t + 1) * P)
+                    matmul(banks[c, b][:, t - pair.start, :], w_q[:, rows], w_sc[:, rows], z_q[:], z_sc[:])
 
         def planes(c):
-            h, lo = divmod(c * n, HALF)
+            h, lo = divmod(c * CHUNK, HALF)
             nc.vector.quantize_mx(
-                out=y_words[h][:, lo : lo + n].bitcast(FP8X4),
-                scales=y_sc[:, c * n : (c + 1) * n],
+                out=y_words[h][:, lo : lo + CHUNK].bitcast(FP8X4),
+                scales=y_sc[:, c * CHUNK : (c + 1) * CHUNK],
                 in_=y_bf[c][:].rearrange("p j t -> p (j t)"),
             )
 
         def store_words(h):
             nc.sync.dma_start(words_of(out_1)[:, h * HALF : (h + 1) * HALF], y_words[h][:].bitcast(I32))
 
-        z_rows = sb([P, PACK, n], BF16, "z_rows")
-        for t in range(PACK):
-            nc.scalar.activation(z_rows[:, t, :], sig[:, 1, t, HALF - n :], ACT.Copy, scale=gn_t[:, t : t + 1])
-        interleave(nc.scalar.copy, z[3][:].rearrange("p (j t) -> p j t", t=PACK), z_rows[:])
-        weigh(0, 0, n)
-        for c, bank_nos in enumerate(((1, 2), (6,))):
-            weigh(c + 1, 0, n // 2)
-            product(c, bank_nos)
-            weigh(c + 1, n // 2, n // 2)
-        product(2, (7,))
-        product(3, (0, 4))
-        for b in range(2):
-            nc.scalar.copy(y[0][:, 2 * b : 2 * b + 2, :], banks[0][b][:])
-            nc.sync.dma_start(out_rows[:, 2 * b : 2 * b + 2, :n], y[0][:, 2 * b : 2 * b + 2, :])
-        nc.scalar.copy(y[1], banks[1][0][:])
-        nc.sync.dma_start(out_rows[:, :, n:HALF], y[1])
-        nc.scalar.copy(y[2], banks[2][0][:])
-        nc.scalar.copy(y_bf[2][:], banks[2][0][:].rearrange("p t j -> p j t"))
-        round_result(0)
+        interleave(nc.scalar.copy, z[2][:], z_rows[:])
+        weigh(0, 0, CHUNK)
+        for ready, following in ((0, 1), (1, 3)):
+            weigh(following, 0, CHUNK // 2)
+            product(ready)
+            weigh(following, CHUNK // 2, CHUNK // 2)
+        product(2)
+        product(3)
+
+        for c in (0, 1):
+            for b, pair in enumerate(pairs):
+                nc.scalar.copy(y[c][:, pair, :], banks[c, b][:])
+                nc.sync.dma_start(out_rows[:, pair, c * CHUNK : (c + 1) * CHUNK], y[c][:, pair, :])
+        for b, pair in enumerate(pairs):
+            nc.scalar.copy(y[2][:, pair, :], banks[2, b][:])
+        interleave(nc.scalar.copy, y_bf[2][:], y[2])
+        interleave(nc.vector.tensor_copy, y_bf[0][:], y[0])
         planes(0)
-        nc.vector.tensor_copy(y[3][:, :2, :], banks[3][0][:])
-        nc.vector.tensor_copy(y[3][:, 2:, :], banks[3][1][:])
-        nc.sync.dma_start(out_rows[:, :, HALF:], y_late[:])
-        round_result(1)
-        round_result(3)
+        for b, pair in enumerate(pairs):
+            nc.vector.tensor_copy(y[3][:, pair, :], banks[3, b][:])
+            nc.sync.dma_start(out_rows[:, pair, HALF:], y_late[:, pair, :])
+        interleave(nc.vector.tensor_copy, y_bf[1][:], y[1])
+        interleave(nc.vector.tensor_copy, y_bf[3][:], y[3])
         planes(1)
         store_words(0)
-        planes(2)
         planes(3)
+        planes(2)
         store_words(1)
         for q in range(4):
-            eng = nc.sync if q % 2 else nc.scalar
-            eng.dma_start(out_2[0, 4 * q : 4 * q + 4, :].bitcast(I32), y_sc[32 * q : 32 * q + 4, :].bitcast(I32))
+            queue = nc.sync if q % 2 else nc.scalar
+            queue.dma_start(out_2[0, 4 * q : 4 * q + 4, :].bitcast(I32), y_sc[32 * q : 32 * q + 4, :].bitcast(I32))

@@ -67,9 +67,9 @@ def tile_picked_scorebias_sigmoid_po_kernel(
         def load_spread(plane, dram):
             nc.sync.dma_start(plane[0:P:8, :].bitcast(I32), dram[0].bitcast(I32))
 
-        def close_up(plane):
-            for r in range(1, 4):
-                nc.sync.dma_start(plane[r:P:32, :].bitcast(I32), plane[8 * r : P : 32, :].bitcast(I32))
+        def close_up(plane, spread, rows):
+            for r in rows:
+                nc.sync.dma_start(plane[r:P:32, :].bitcast(I32), spread[8 * r : P : 32, :].bitcast(I32))
 
         def matmul(out, lhsT, lhsT_scale, rhs, rhs_scale):
             nc.tensor.matmul_mx(
@@ -84,21 +84,18 @@ def tile_picked_scorebias_sigmoid_po_kernel(
 
         tab_bytes = 4 * U
         at_w_raw = 0
-        at_w_sc_raw = at_w_raw + 4 * N
-        at_tab0 = at_w_sc_raw + N
-        at_d_win = at_tab0 + tab_bytes
-        at_x_sc_win = at_d_win + 4 * G
-        at_w_q = at_x_sc_win + tab_bytes
-        at_gn = at_w_q + 4 * N
-        at_tab3 = at_gn + ALIGN
+        at_tab = [4 * N + t * tab_bytes for t in range(PACK)]
+        at_gn = at_tab[-1] + tab_bytes
+        at_d_got = at_gn + ALIGN
+        at_x_win = at_d_got + 4 * S
 
         kidx_t = keep.tile([P, H // GROUP], U16, name="kidx_t")
         offs_t = keep.tile([P, S // GROUP], U16, name="offs_t")
         rel_t = keep.tile([P, S // GROUP], U16, name="rel_t")
         d_sc_win = sb([P, G], U8, "d_sc_win")
-        x_sc_win = placed([P, T], U8, "x_sc_win", at_x_sc_win)
-        d_win = placed([P, G], U32, "d_win", at_d_win)
-        x_win = sb([P, T], U32, "x_win")
+        x_sc_win = sb([P, T], U8, "x_sc_win")
+        d_win = sb([P, G], U32, "d_win")
+        x_win = placed([P, T], U32, "x_win", at_x_win)
 
         tab_rows = tab.rearrange("(p t) u -> p t u", t=PACK)
         tab_t = []
@@ -108,19 +105,24 @@ def tile_picked_scorebias_sigmoid_po_kernel(
             tab_t.append(placed([P, U], F32, "tab%d" % t, offset))
             nc.sync.dma_start(tab_t[t][:], tab_rows[:, t, :])
 
-        nc.vector.memset(d_sc_win[:].bitcast(I32), 0)
-        nc.vector.memset(x_sc_win[:, : T // 2].bitcast(I32), 0)
-        nc.gpsimd.memset(x_sc_win[:, T // 2 :].bitcast(I32), 0)
+        nc.gpsimd.memset(d_sc_win[:].bitcast(I32), 0)
+        nc.vector.memset(x_sc_win[:].bitcast(I32), 0)
         warm = sb([P, 2], F32, "warm")
         nc.gpsimd.memset(warm[:, 0:1], 0.0)
         nc.scalar.activation(warm[:, 1:2], warm[:, 0:1], ACT.Sigmoid)
 
         early = G // 4
+        w_sc_raw = sb([P, N], U8, "w_sc_raw")
+        nc.sync.dma_start(
+            w_sc_raw[:].bitcast(I32), w1_scales[0].bitcast(I32).unsqueeze(1).to_broadcast([16, 8, N // 4])
+        )
+        w_sc_dealt = sb([P, N], U8, "w_sc_dealt")
+        deal(nc, w_sc_dealt[:], w_sc_raw[:], 0)
         nc.sync.dma_start(kidx_t[:], kidx)
-        nc.sync.dma_start(offs_t[:], offs)
         nc.sync.dma_start(d_win[:, :early].bitcast(I32), words_of(d_words)[:, :early])
         load_spread(d_sc_win, d_scales)
         nc.sync.dma_start(d_win[:, early:].bitcast(I32), words_of(d_words)[:, early:])
+        nc.sync.dma_start(offs_t[:], offs)
         for q in range(4):
             nc.sync.dma_start(x_sc_win[32 * q : 32 * q + 4, :].bitcast(I32), x_scales[0, 4 * q : 4 * q + 4, :].bitcast(I32))
         nc.sync.dma_start(x_win[:].bitcast(I32), words_of(x_words))
@@ -133,38 +135,28 @@ def tile_picked_scorebias_sigmoid_po_kernel(
                 deal(nc, dealt[:].bitcast(move_as), got.bitcast(move_as), h * HALF)
 
         d_sc = sb([P, H], U8, "d_sc")
-        d_sc_hold = placed([P, N + 2 * ALIGN], U8, "d_sc_got1", at_w_sc_raw - ALIGN)
+        d_sc_hold = placed([P, at_d_got], U8, "d_sc_got1", 0)
         pick_keys(d_sc, (sb([P, HALF], U8, "d_sc_got0")[:], d_sc_hold[:, :HALF]), d_sc_win, U8)
-        close_up(d_sc)
+        close_up(d_sc, d_sc, range(1, 4))
         w_raw = placed([P, N], U32, "w_raw", at_w_raw)
         nc.sync.dma_start(w_raw[:].bitcast(I32), words_of(w1_words))
-        load_tab(at_tab0)
-        w_sc_raw = placed([P, N], U8, "w_sc_raw", at_w_sc_raw)
-        nc.gpsimd.memset(w_sc_raw[:].bitcast(I32), 0)
-        load_spread(w_sc_raw, w1_scales)
-
-        d_q = sb([P, H], U32, "d_q")
-        d_hold = placed([P, HALF], U32, "d_got1", at_gn - ALIGN)
-        pick_keys(d_q, (sb([P, HALF], U32, "d_got0")[:], d_hold[:]), d_win, I32)
-        load_tab(at_d_win)
-        x_sc = sb([P, S], U8, "x_sc")
-        nc.vector.tensor_copy(x_sc[:], x_sc_win[:].indirect(offs_t[:]))
-        load_tab(at_x_sc_win)
-        load_tab(at_tab3)
+        for offset in at_tab:
+            load_tab(offset)
         gn_t = placed([P, PACK], F32, "gn_t", at_gn)
         nc.sync.dma_start(gn_t[:], gn.rearrange("(p t) o -> p (t o)", t=PACK))
 
+        x_sc = sb([P, S], U8, "x_sc")
+        nc.vector.tensor_copy(x_sc[:], x_sc_win[:].indirect(offs_t[:]))
+        d_q = sb([P, H], U32, "d_q")
+        pick_keys(d_q, (sb([P, HALF], U32, "d_got0")[:], sb([P, HALF], U32, "d_got1")[:]), d_win, I32)
         x_q = [sb([P, HALF], U32, "x_q%d" % h) for h in range(2)]
         for h in range(2):
             nc.vector.tensor_copy(x_q[h][:], x_win[:].indirect(entries(offs_t, h * HALF, HALF)))
-        w_q = placed([P, N], U32, "w_q", at_w_q)
-        w_sc = sb([P, N], U8, "w_sc")
+        w_q = placed([P, N], U32, "w_q", at_x_win)
         deal(nc, w_q[:].bitcast(I32), w_raw[:].bitcast(I32), 0)
-        deal(nc, w_sc[:], w_sc_raw[:], 0)
-        close_up(w_sc)
 
         score = [sb([P, S], F32, "score%d" % t) for t in range(PACK)]
-        biased = [placed([P, S], F32, "biased0", at_tab0 - 4 * S)]
+        biased = [placed([P, S], F32, "biased0", at_d_got)]
         biased.extend(sb([P, S], F32, "biased%d" % t) for t in range(1, PACK))
         sig = sb([P, 2, PACK, HALF], F32, "sig")
         z_rows = sb([P, PACK, CHUNK], BF16, "z_rows")
@@ -198,6 +190,10 @@ def tile_picked_scorebias_sigmoid_po_kernel(
             add_biases(0, first, HALF)
             sigmoids(0, first, HALF)
         weigh_on_scalar(0)
+        w_sc = placed([P, N], U8, "w_sc", at_d_got)
+        close_up(w_sc, w_sc_dealt, range(4))
+        for number in (1, 2):
+            matmul(bank_tile([P, N], number, "warm_bank%d" % number)[:], w_q[:, :P], w_sc[:, :P], w_q[:], w_sc[:])
         for t in (1, 2):
             add_biases(t, 0, S)
             sigmoids(t, HALF, HALF)

@@ -21,7 +21,7 @@ GROUP = 16
 HALF = 256
 CHUNK = 128
 PAIR = 2
-LINE = 4
+RUN = 8
 BANKS = 8
 ALIGN = 64
 
@@ -34,16 +34,18 @@ def entries(list_tile, first, count):
     return list_tile[:, first // GROUP : (first + count) // GROUP]
 
 
-def deal(nc, dst, src, first):
-    runs = slice(first // (PACK * LINE), (first + src.shape[1]) // (PACK * LINE))
+def deal(nc, dst, src, first, size):
+    run = RUN // size
+    runs = slice(first // (PACK * run), (first + src.shape[1]) // (PACK * run))
     nc.vector.tensor_copy(
-        dst.rearrange("p (t g i) -> p g t i", t=PACK, i=LINE)[:, runs],
-        src.rearrange("p (g i t) -> p g t i", t=PACK, i=LINE),
+        dst.rearrange("p (t g i) -> p g t i", t=PACK, i=run)[:, runs],
+        src.rearrange("p (g i t) -> p g t i", t=PACK, i=run),
     )
 
 
-def interleave(copy, dst, src):
-    copy(dst.rearrange("p (g i) t -> p g t i", i=LINE), src.rearrange("p t (g i) -> p g t i", i=LINE))
+def interleave(copy, dst, src, size):
+    run = RUN // size
+    copy(dst.rearrange("p (g i) t -> p g t i", i=run), src.rearrange("p t (g i) -> p g t i", i=run))
 
 
 def tile_picked_scorebias_sigmoid_po_kernel(
@@ -117,7 +119,7 @@ def tile_picked_scorebias_sigmoid_po_kernel(
             w_sc_raw[:].bitcast(I32), w1_scales[0].bitcast(I32).unsqueeze(1).to_broadcast([16, 8, N // 4])
         )
         w_sc_dealt = sb([P, N], U8, "w_sc_dealt")
-        deal(nc, w_sc_dealt[:], w_sc_raw[:], 0)
+        deal(nc, w_sc_dealt[:], w_sc_raw[:], 0, 1)
         nc.sync.dma_start(kidx_t[:], kidx)
         nc.sync.dma_start(d_win[:, :early].bitcast(I32), words_of(d_words)[:, :early])
         load_spread(d_sc_win, d_scales)
@@ -128,15 +130,15 @@ def tile_picked_scorebias_sigmoid_po_kernel(
         nc.sync.dma_start(x_win[:].bitcast(I32), words_of(x_words))
         nc.sync.dma_start(rel_t[:], rel)
 
-        def pick_keys(dealt, halves, window, move_as):
+        def pick_keys(dealt, halves, window, move_as, size):
             for h, got in enumerate(halves):
                 nc.vector.tensor_copy(got, window[:].indirect(entries(kidx_t, h * HALF, HALF)))
             for h, got in enumerate(halves):
-                deal(nc, dealt[:].bitcast(move_as), got.bitcast(move_as), h * HALF)
+                deal(nc, dealt[:].bitcast(move_as), got.bitcast(move_as), h * HALF, size)
 
         d_sc = sb([P, H], U8, "d_sc")
         d_sc_hold = placed([P, at_d_got], U8, "d_sc_got1", 0)
-        pick_keys(d_sc, (sb([P, HALF], U8, "d_sc_got0")[:], d_sc_hold[:, :HALF]), d_sc_win, U8)
+        pick_keys(d_sc, (sb([P, HALF], U8, "d_sc_got0")[:], d_sc_hold[:, :HALF]), d_sc_win, U8, 1)
         close_up(d_sc, d_sc, range(1, 4))
         w_raw = placed([P, N], U32, "w_raw", at_w_raw)
         nc.sync.dma_start(w_raw[:].bitcast(I32), words_of(w1_words))
@@ -148,12 +150,12 @@ def tile_picked_scorebias_sigmoid_po_kernel(
         x_sc = sb([P, S], U8, "x_sc")
         nc.vector.tensor_copy(x_sc[:], x_sc_win[:].indirect(offs_t[:]))
         d_q = sb([P, H], U32, "d_q")
-        pick_keys(d_q, (sb([P, HALF], U32, "d_got0")[:], sb([P, HALF], U32, "d_got1")[:]), d_win, I32)
+        pick_keys(d_q, (sb([P, HALF], U32, "d_got0")[:], sb([P, HALF], U32, "d_got1")[:]), d_win, I32, 4)
         x_q = [sb([P, HALF], U32, "x_q%d" % h) for h in range(2)]
         for h in range(2):
             nc.vector.tensor_copy(x_q[h][:], x_win[:].indirect(entries(offs_t, h * HALF, HALF)))
         w_q = placed([P, N], U32, "w_q", at_x_win)
-        deal(nc, w_q[:].bitcast(I32), w_raw[:].bitcast(I32), 0)
+        deal(nc, w_q[:].bitcast(I32), w_raw[:].bitcast(I32), 0, 4)
 
         score = [sb([P, S], F32, "score%d" % t) for t in range(PACK)]
         biased = [placed([P, S], F32, "biased0", at_d_got)]
@@ -219,10 +221,11 @@ def tile_picked_scorebias_sigmoid_po_kernel(
 
         def weigh(c, lo, count):
             h, first = divmod(c * CHUNK + lo, HALF)
+            run = RUN // 4
             nc.vector.tensor_tensor(
-                z[c][:, lo : lo + count, :].rearrange("p (g i) t -> p g t i", i=LINE),
-                sig[:, h, :, first : first + count].rearrange("p t (g i) -> p g t i", i=LINE),
-                gn_t[:].unsqueeze(1).unsqueeze(3).to_broadcast([P, count // LINE, PACK, LINE]),
+                z[c][:, lo : lo + count, :].rearrange("p (g i) t -> p g t i", i=run),
+                sig[:, h, :, first : first + count].rearrange("p t (g i) -> p g t i", i=run),
+                gn_t[:].unsqueeze(1).unsqueeze(3).to_broadcast([P, count // run, PACK, run]),
                 ALU.mult,
             )
 
@@ -247,7 +250,7 @@ def tile_picked_scorebias_sigmoid_po_kernel(
         def store_words(h):
             nc.sync.dma_start(words_of(out_1)[:, h * HALF : (h + 1) * HALF], y_words[h][:].bitcast(I32))
 
-        interleave(nc.scalar.copy, z[2][:], z_rows[:])
+        interleave(nc.scalar.copy, z[2][:], z_rows[:], 2)
         weigh(0, 0, CHUNK)
         for ready, following in ((0, 1), (1, 3)):
             weigh(following, 0, CHUNK // 2)
@@ -262,14 +265,14 @@ def tile_picked_scorebias_sigmoid_po_kernel(
                 nc.sync.dma_start(out_rows[:, pair, c * CHUNK : (c + 1) * CHUNK], y[c][:, pair, :])
         for b, pair in enumerate(pairs):
             nc.scalar.copy(y[2][:, pair, :], banks[2, b][:])
-        interleave(nc.scalar.copy, y_bf[2][:], y[2])
-        interleave(nc.vector.tensor_copy, y_bf[0][:], y[0])
+        interleave(nc.scalar.copy, y_bf[2][:], y[2], 4)
+        interleave(nc.vector.tensor_copy, y_bf[0][:], y[0], 4)
         planes(0)
         for b, pair in enumerate(pairs):
             nc.vector.tensor_copy(y[3][:, pair, :], banks[3, b][:])
             nc.sync.dma_start(out_rows[:, pair, HALF:], y_late[:, pair, :])
-        interleave(nc.vector.tensor_copy, y_bf[1][:], y[1])
-        interleave(nc.vector.tensor_copy, y_bf[3][:], y[3])
+        interleave(nc.vector.tensor_copy, y_bf[1][:], y[1], 4)
+        interleave(nc.vector.tensor_copy, y_bf[3][:], y[3], 4)
         planes(1)
         store_words(0)
         planes(3)

@@ -89,7 +89,6 @@ def tile_picked_scorebias_sigmoid_po_kernel(
         at_tab = [4 * N + t * tab_bytes for t in range(PACK)]
         at_gn = at_tab[-1] + tab_bytes
         at_d_got = at_gn + ALIGN
-        at_x_win = at_d_got + 4 * S
 
         kidx_t = keep.tile([P, H // GROUP], U16, name="kidx_t")
         offs_t = keep.tile([P, S // GROUP], U16, name="offs_t")
@@ -97,7 +96,7 @@ def tile_picked_scorebias_sigmoid_po_kernel(
         d_sc_win = sb([P, G], U8, "d_sc_win")
         x_sc_win = sb([P, T], U8, "x_sc_win")
         d_win = sb([P, G], U32, "d_win")
-        x_win = placed([P, T], U32, "x_win", at_x_win)
+        x_win = sb([P, T], U32, "x_win")
 
         tab_rows = tab.rearrange("(p t) u -> p t u", t=PACK)
         tab_t = []
@@ -140,9 +139,10 @@ def tile_picked_scorebias_sigmoid_po_kernel(
         d_sc_hold = placed([P, at_d_got], U8, "d_sc_got1", 0)
         pick_keys(d_sc, (sb([P, HALF], U8, "d_sc_got0")[:], d_sc_hold[:, :HALF]), d_sc_win, U8, 1)
         close_up(d_sc, d_sc, range(1, 4))
+        load_tab(at_tab[0])
         w_raw = placed([P, N], U32, "w_raw", at_w_raw)
         nc.sync.dma_start(w_raw[:].bitcast(I32), words_of(w1_words))
-        for offset in at_tab:
+        for offset in at_tab[1:]:
             load_tab(offset)
         gn_t = placed([P, PACK], F32, "gn_t", at_gn)
         nc.sync.dma_start(gn_t[:], gn.rearrange("(p t) o -> p (t o)", t=PACK))
@@ -154,12 +154,10 @@ def tile_picked_scorebias_sigmoid_po_kernel(
         x_q = [sb([P, HALF], U32, "x_q%d" % h) for h in range(2)]
         for h in range(2):
             nc.vector.tensor_copy(x_q[h][:], x_win[:].indirect(entries(offs_t, h * HALF, HALF)))
-        w_q = placed([P, N], U32, "w_q", at_x_win)
-        deal(nc, w_q[:].bitcast(I32), w_raw[:].bitcast(I32), 0, 4)
 
-        score = [sb([P, S], F32, "score%d" % t) for t in range(PACK)]
-        biased = [placed([P, S], F32, "biased0", at_d_got)]
-        biased.extend(sb([P, S], F32, "biased%d" % t) for t in range(1, PACK))
+        score = {t: sb([P, S], F32, "score%d" % t) for t in range(1, PACK)}
+        biased = {t: sb([P, S], F32, "biased%d" % t) for t in range(1, PACK)}
+        biased0 = [placed([P, HALF], F32, "biased0_0", at_d_got), sb([P, HALF], F32, "biased0_1")]
         sig = sb([P, 2, PACK, HALF], F32, "sig")
         z_rows = sb([P, PACK, CHUNK], BF16, "z_rows")
 
@@ -169,7 +167,7 @@ def tile_picked_scorebias_sigmoid_po_kernel(
             for lo in range(0, count, HALF):
                 cols = slice(first + lo, first + lo + HALF)
                 matmul(bank[:, lo : lo + HALF], d_q[:, keys], d_sc[:, keys], x_q[cols.start // HALF][:], x_sc[:, cols])
-            nc.scalar.activation(score[t][:, first : first + count], bank[:], ACT.Copy, scale=0.0625)
+            return bank
 
         def add_biases(t, first, count):
             cols = slice(first, first + count)
@@ -184,13 +182,20 @@ def tile_picked_scorebias_sigmoid_po_kernel(
         def weigh_on_scalar(t):
             nc.scalar.activation(z_rows[:, t, :], sig[:, 1, t, :CHUNK], ACT.Copy, scale=gn_t[:, t : t + 1])
 
-        scores(0, 0, HALF, 0)
-        scores(0, HALF, HALF, PACK)
-        for t in range(1, PACK):
-            scores(t, 0, S, t)
-        for first in (0, HALF):
-            add_biases(0, first, HALF)
-            sigmoids(0, first, HALF)
+        nc.scalar.activation(score[1][:], scores(1, 0, S, 1)[:], ACT.Copy, scale=0.0625)
+        first_banks = [scores(0, 0, HALF, 0), scores(0, HALF, HALF, PACK)]
+        for t in range(2, PACK):
+            nc.scalar.activation(score[t][:], scores(t, 0, S, t)[:], ACT.Copy, scale=0.0625)
+        bias0 = [sb([P, HALF], F32, "bias0_%d" % h) for h in range(2)]
+        for h in range(2):
+            nc.vector.tensor_copy(bias0[h][:], tab_t[0][:].indirect(entries(rel_t, h * HALF, HALF)))
+        for h in range(2):
+            nc.vector.scalar_tensor_tensor(
+                biased0[h][:], first_banks[h][:], 0.0625, bias0[h][:], ALU.mult, ALU.add
+            )
+            nc.scalar.activation(sig[:, h, 0, :], biased0[h][:], ACT.Sigmoid)
+        w_q = sb([P, N], U32, "w_q")
+        deal(nc, w_q[:].bitcast(I32), w_raw[:].bitcast(I32), 0, 4)
         weigh_on_scalar(0)
         w_sc = placed([P, N], U8, "w_sc", at_d_got)
         close_up(w_sc, w_sc_dealt, range(4))

@@ -195,7 +195,7 @@ def tile_picked_scorebias_sigmoid_po_kernel(
             )
             nc.scalar.activation(sig[:, h, 0, :], biased0[h][:], ACT.Sigmoid)
         w_q = sb([P, N], U32, "w_q")
-        deal(nc, w_q[:].bitcast(I32), w_raw[:].bitcast(I32), 0, 4)
+        nc.gpsimd.tensor_copy(w_q[:].rearrange("p (t m) -> p t m", t=PACK), w_raw[:].rearrange("p (m t) -> p t m", t=PACK))
         weigh_on_scalar(0)
         w_sc = placed([P, N], U8, "w_sc", at_d_got)
         close_up(w_sc, w_sc_dealt, range(4))

@@ -69,9 +69,9 @@ def tile_picked_scorebias_sigmoid_po_kernel(
         def load_spread(plane, dram):
             nc.sync.dma_start(plane[0:P:8, :].bitcast(I32), dram[0].bitcast(I32))
 
-        def close_up(plane, spread, rows):
+        def close_up(queue, plane, spread, rows):
             for r in rows:
-                nc.sync.dma_start(plane[r:P:32, :].bitcast(I32), spread[8 * r : P : 32, :].bitcast(I32))
+                queue.dma_start(plane[r:P:32, :].bitcast(I32), spread[8 * r : P : 32, :].bitcast(I32))
 
         def matmul(out, lhsT, lhsT_scale, rhs, rhs_scale):
             nc.tensor.matmul_mx(
@@ -86,9 +86,12 @@ def tile_picked_scorebias_sigmoid_po_kernel(
 
         tab_bytes = 4 * U
         at_w_raw = 0
-        at_tab = [4 * N + t * tab_bytes for t in range(PACK)]
-        at_gn = at_tab[-1] + tab_bytes
-        at_d_got = at_gn + ALIGN
+        at_gn = 4 * N
+        at_tab = [at_gn + ALIGN + 4 * tab_bytes] + [at_gn + ALIGN + t * tab_bytes for t in range(PACK - 1)]
+        at_d_got = at_tab[0] + tab_bytes + ALIGN
+        at_score2 = at_tab[0] - 4 * S + ALIGN
+        at_score1 = at_tab[0] + ALIGN
+        at_score3 = at_score1 + 4 * S
 
         kidx_t = keep.tile([P, H // GROUP], U16, name="kidx_t")
         offs_t = keep.tile([P, S // GROUP], U16, name="offs_t")
@@ -122,12 +125,14 @@ def tile_picked_scorebias_sigmoid_po_kernel(
         nc.sync.dma_start(kidx_t[:], kidx)
         nc.sync.dma_start(d_win[:, :early].bitcast(I32), words_of(d_words)[:, :early])
         load_spread(d_sc_win, d_scales)
-        nc.sync.dma_start(d_win[:, early:].bitcast(I32), words_of(d_words)[:, early:])
         nc.sync.dma_start(offs_t[:], offs)
-        for q in range(4):
-            nc.sync.dma_start(x_sc_win[32 * q : 32 * q + 4, :].bitcast(I32), x_scales[0, 4 * q : 4 * q + 4, :].bitcast(I32))
+        load_spread(x_sc_win, x_scales)
+        nc.sync.dma_start(d_win[:, early:].bitcast(I32), words_of(d_words)[:, early:])
         nc.sync.dma_start(x_win[:].bitcast(I32), words_of(x_words))
         nc.sync.dma_start(rel_t[:], rel)
+        load_tab(at_tab[0])
+        w_raw = sb([P, N], U32, "w_raw")
+        nc.sync.dma_start(w_raw[:].bitcast(I32), words_of(w1_words))
 
         def pick_keys(dealt, halves, window, move_as, size):
             for h, got in enumerate(halves):
@@ -135,31 +140,31 @@ def tile_picked_scorebias_sigmoid_po_kernel(
             for h, got in enumerate(halves):
                 deal(nc, dealt[:].bitcast(move_as), got.bitcast(move_as), h * HALF, size)
 
-        d_sc = sb([P, H], U8, "d_sc")
-        d_sc_hold = placed([P, at_d_got], U8, "d_sc_got1", 0)
-        pick_keys(d_sc, (sb([P, HALF], U8, "d_sc_got0")[:], d_sc_hold[:, :HALF]), d_sc_win, U8, 1)
-        close_up(d_sc, d_sc, range(1, 4))
-        load_tab(at_tab[0])
-        w_raw = placed([P, N], U32, "w_raw", at_w_raw)
-        nc.sync.dma_start(w_raw[:].bitcast(I32), words_of(w1_words))
+        picked_sc = sb([P, H + S], U8, "picked_sc")
+        d_sc, x_sc = picked_sc[:, :H], picked_sc[:, H:]
+        d_sc_got = sb([P, H], U8, "d_sc_got")
+        x_sc_got = placed([P, at_score2], U8, "x_sc_got", 0)
+        nc.vector.tensor_copy(d_sc_got[:], d_sc_win[:].indirect(kidx_t[:]))
+        nc.vector.tensor_copy(x_sc_got[:, :S], x_sc_win[:].indirect(offs_t[:]))
+        deal(nc, d_sc, d_sc_got[:], 0, 1)
+        nc.vector.tensor_copy(x_sc.bitcast(I32), x_sc_got[:, :S].bitcast(I32))
+        close_up(nc.sync, picked_sc, picked_sc, range(1, 4))
         for offset in at_tab[1:]:
             load_tab(offset)
         gn_t = placed([P, PACK], F32, "gn_t", at_gn)
         nc.sync.dma_start(gn_t[:], gn.rearrange("(p t) o -> p (t o)", t=PACK))
 
-        x_sc = sb([P, S], U8, "x_sc")
-        nc.vector.tensor_copy(x_sc[:], x_sc_win[:].indirect(offs_t[:]))
         d_q = sb([P, H], U32, "d_q")
         pick_keys(d_q, (sb([P, HALF], U32, "d_got0")[:], sb([P, HALF], U32, "d_got1")[:]), d_win, I32, 4)
         x_q = [sb([P, HALF], U32, "x_q%d" % h) for h in range(2)]
         for h in range(2):
             nc.vector.tensor_copy(x_q[h][:], x_win[:].indirect(entries(offs_t, h * HALF, HALF)))
 
-        score = {t: sb([P, S], F32, "score%d" % t) for t in range(1, PACK)}
+        last = PACK - 1
+        half_bytes = 4 * HALF
         biased = {t: sb([P, S], F32, "biased%d" % t) for t in range(1, PACK)}
-        biased0 = [placed([P, HALF], F32, "biased0_0", at_d_got), sb([P, HALF], F32, "biased0_1")]
+        biased0 = [sb([P, HALF], F32, "biased0_0"), sb([P, HALF], F32, "biased0_1")]
         sig = sb([P, 2, PACK, HALF], F32, "sig")
-        z_rows = sb([P, PACK, CHUNK], BF16, "z_rows")
 
         def scores(t, first, count, bank_number):
             bank = bank_tile([P, count], bank_number, "score_bank%d" % bank_number)
@@ -169,49 +174,55 @@ def tile_picked_scorebias_sigmoid_po_kernel(
                 matmul(bank[:, lo : lo + HALF], d_q[:, keys], d_sc[:, keys], x_q[cols.start // HALF][:], x_sc[:, cols])
             return bank
 
-        def add_biases(t, first, count):
-            cols = slice(first, first + count)
-            nc.vector.tensor_tensor(
-                biased[t][:, cols], tab_t[t][:].indirect(entries(rel_t, first, count)), score[t][:, cols], ALU.add
-            )
+        def copied(t, first, count, bank_number, offset):
+            tile = placed([P, count], F32, "score%d_%d" % (t, first), offset)
+            nc.scalar.activation(tile[:], scores(t, first, count, bank_number)[:], ACT.Copy, scale=0.0625)
+            return tile
 
-        def sigmoids(t, first, count):
-            h, lo = divmod(first, HALF)
-            nc.scalar.activation(sig[:, h, t, lo : lo + count], biased[t][:, first : first + count], ACT.Sigmoid)
+        def window(t, first, count):
+            return tab_t[t][:].indirect(entries(rel_t, first, count))
 
-        def weigh_on_scalar(t):
-            nc.scalar.activation(z_rows[:, t, :], sig[:, 1, t, :CHUNK], ACT.Copy, scale=gn_t[:, t : t + 1])
+        def add_biases(t, first, score):
+            count = score.shape[1]
+            nc.vector.tensor_tensor(biased[t][:, first : first + count], window(t, first, count), score[:], ALU.add)
 
-        nc.scalar.activation(score[1][:], scores(1, 0, S, 1)[:], ACT.Copy, scale=0.0625)
-        first_banks = [scores(0, 0, HALF, 0), scores(0, HALF, HALF, PACK)]
-        for t in range(2, PACK):
-            nc.scalar.activation(score[t][:], scores(t, 0, S, t)[:], ACT.Copy, scale=0.0625)
         bias0 = [sb([P, HALF], F32, "bias0_%d" % h) for h in range(2)]
         for h in range(2):
-            nc.vector.tensor_copy(bias0[h][:], tab_t[0][:].indirect(entries(rel_t, h * HALF, HALF)))
+            nc.scalar.activation(bias0[h][:], window(0, h * HALF, HALF), ACT.Copy)
+        first_banks = [scores(0, 0, HALF, 0)]
+        score1 = [copied(1, 0, HALF, 1, at_score1)]
+        first_banks.append(scores(0, HALF, HALF, 4))
+        score1.append(copied(1, HALF, HALF, 5, at_score1 + half_bytes))
         for h in range(2):
             nc.vector.scalar_tensor_tensor(
                 biased0[h][:], first_banks[h][:], 0.0625, bias0[h][:], ALU.mult, ALU.add
             )
-            nc.scalar.activation(sig[:, h, 0, :], biased0[h][:], ACT.Sigmoid)
+        nc.scalar.activation(sig[:, 0, 0, :], biased0[0][:], ACT.Sigmoid)
+        score2 = copied(2, 0, S, 2, at_score2)
+        nc.scalar.activation(sig[:, 1, 0, :], biased0[1][:], ACT.Sigmoid)
+        score3 = [copied(last, h * HALF, HALF, (3, 6)[h], at_score3 + h * half_bytes) for h in range(2)]
         w_q = sb([P, N], U32, "w_q")
         nc.gpsimd.tensor_copy(w_q[:].rearrange("p (t m) -> p t m", t=PACK), w_raw[:].rearrange("p (m t) -> p t m", t=PACK))
-        weigh_on_scalar(0)
-        w_sc = placed([P, N], U8, "w_sc", at_d_got)
-        close_up(w_sc, w_sc_dealt, range(4))
+        for h in range(2):
+            add_biases(1, h * HALF, score1[h])
+        w_sc = placed([P, N], U8, "w_sc", at_score1 + half_bytes)
+        close_up(nc.sync, w_sc, w_sc_dealt, range(4))
         for number in (1, 2):
             matmul(bank_tile([P, N], number, "warm_bank%d" % number)[:], w_q[:, :P], w_sc[:, :P], w_q[:], w_sc[:])
+        add_biases(2, 0, score2)
         for t in (1, 2):
-            add_biases(t, 0, S)
-            sigmoids(t, HALF, HALF)
-            sigmoids(t, 0, HALF)
+            nc.scalar.activation(sig[:, :, t, :], biased[t][:].rearrange("p (h j) -> p h j", h=2), ACT.Sigmoid)
+        add_biases(last, 0, score3[0])
+        nc.scalar.activation(sig[:, 0, last, :], biased[last][:, :HALF], ACT.Sigmoid)
+        add_biases(last, HALF, score3[1])
+        z_rows = placed([P, PACK, CHUNK], BF16, "z_rows", at_score3)
+
+        def weigh_on_scalar(t):
+            nc.scalar.activation(z_rows[:, t, :], sig[:, 1, t, :CHUNK], ACT.Copy, scale=gn_t[:, t : t + 1])
+
+        nc.scalar.activation(sig[:, 1, last, :], biased[last][:, HALF:], ACT.Sigmoid)
+        for t in range(PACK):
             weigh_on_scalar(t)
-        add_biases(3, 0, HALF)
-        sigmoids(3, 0, HALF)
-        add_biases(3, HALF, HALF)
-        sigmoids(3, HALF, CHUNK)
-        sigmoids(3, HALF + CHUNK, CHUNK)
-        weigh_on_scalar(3)
 
         chunks = range(S // CHUNK)
         pairs = [slice(lo, lo + PAIR) for lo in range(0, PACK, PAIR)]
@@ -239,7 +250,7 @@ def tile_picked_scorebias_sigmoid_po_kernel(
             z_sc = sb([P, CHUNK], U8, "z_sc%d" % c)
             nc.vector.quantize_mx(out=z_q[:].bitcast(FP8X4), scales=z_sc[:], in_=z[c][:].rearrange("p j t -> p (j t)"))
             for b, pair in enumerate(pairs):
-                banks[c, b] = bank_tile([P, PAIR, CHUNK], (PACK + 1 + len(pairs) * c + b) % BANKS, "y_bank%d_%d" % (c, b))
+                banks[c, b] = bank_tile([P, PAIR, CHUNK], (BANKS - 1 + len(pairs) * c + b) % BANKS, "y_bank%d_%d" % (c, b))
                 for t in range(pair.start, pair.stop):
                     rows = slice(t * P, (t + 1) * P)
                     matmul(banks[c, b][:, t - pair.start, :], w_q[:, rows], w_sc[:, rows], z_q[:], z_sc[:])

@@ -130,9 +130,9 @@ def tile_picked_scorebias_sigmoid_po_kernel(
         nc.sync.dma_start(d_win[:, early:].bitcast(I32), words_of(d_words)[:, early:])
         nc.sync.dma_start(x_win[:].bitcast(I32), words_of(x_words))
         nc.sync.dma_start(rel_t[:], rel)
-        load_tab(at_tab[0])
         w_raw = sb([P, N], U32, "w_raw")
         nc.sync.dma_start(w_raw[:].bitcast(I32), words_of(w1_words))
+        load_tab(at_tab[0])
 
         def pick_keys(dealt, halves, window, move_as, size):
             for h, got in enumerate(halves):
@@ -187,8 +187,12 @@ def tile_picked_scorebias_sigmoid_po_kernel(
             nc.vector.tensor_tensor(biased[t][:, first : first + count], window(t, first, count), score[:], ALU.add)
 
         bias0 = [sb([P, HALF], F32, "bias0_%d" % h) for h in range(2)]
-        for h in range(2):
-            nc.scalar.activation(bias0[h][:], window(0, h * HALF, HALF), ACT.Copy)
+        w_q = sb([P, N], U32, "w_q")
+        nc.scalar.copy(
+            w_q[:].rearrange("p (t g i) -> p g t i", t=PACK, i=PACK), w_raw[:].rearrange("p (g i t) -> p g t i", t=PACK, i=PACK)
+        )
+        nc.scalar.activation(bias0[0][:], window(0, 0, HALF), ACT.Copy)
+        nc.vector.tensor_copy(bias0[1][:], window(0, HALF, HALF))
         first_banks = [scores(0, 0, HALF, 0)]
         score1 = [copied(1, 0, HALF, 1, at_score1)]
         first_banks.append(scores(0, HALF, HALF, 4))
@@ -201,8 +205,6 @@ def tile_picked_scorebias_sigmoid_po_kernel(
         score2 = copied(2, 0, S, 2, at_score2)
         nc.scalar.activation(sig[:, 1, 0, :], biased0[1][:], ACT.Sigmoid)
         score3 = [copied(last, h * HALF, HALF, (3, 6)[h], at_score3 + h * half_bytes) for h in range(2)]
-        w_q = sb([P, N], U32, "w_q")
-        nc.gpsimd.tensor_copy(w_q[:].rearrange("p (t m) -> p t m", t=PACK), w_raw[:].rearrange("p (m t) -> p t m", t=PACK))
         for h in range(2):
             add_biases(1, h * HALF, score1[h])
         w_sc = placed([P, N], U8, "w_sc", at_score1 + half_bytes)

@@ -209,8 +209,8 @@ def tile_picked_scorebias_sigmoid_po_kernel(
             add_biases(1, h * HALF, score1[h])
         w_sc = placed([P, N], U8, "w_sc", at_score1 + half_bytes)
         close_up(nc.sync, w_sc, w_sc_dealt, range(4))
-        for number in (1, 2):
-            matmul(bank_tile([P, N], number, "warm_bank%d" % number)[:], w_q[:, :P], w_sc[:, :P], w_q[:], w_sc[:])
+        for number in (1, 2, 5):
+            matmul(bank_tile([32, N], number, "warm_bank%d" % number)[:], w_q[:, :32], w_sc[:, :32], w_q[:], w_sc[:])
         add_biases(2, 0, score2)
         for t in (1, 2):
             nc.scalar.activation(sig[:, :, t, :], biased[t][:].rearrange("p (h j) -> p h j", h=2), ACT.Sigmoid)

@@ -207,7 +207,7 @@ def tile_picked_scorebias_sigmoid_po_kernel(
         score3 = [copied(last, h * HALF, HALF, (3, 6)[h], at_score3 + h * half_bytes) for h in range(2)]
         for h in range(2):
             add_biases(1, h * HALF, score1[h])
-        w_sc = placed([P, N], U8, "w_sc", at_score1 + half_bytes)
+        w_sc = placed([P, N], U8, "w_sc", at_score1)
         close_up(nc.sync, w_sc, w_sc_dealt, range(4))
         for number in (1, 2, 5):
             matmul(bank_tile([32, N], number, "warm_bank%d" % number)[:], w_q[:, :32], w_sc[:, :32], w_q[:], w_sc[:])

@@ -130,9 +130,9 @@ def tile_picked_scorebias_sigmoid_po_kernel(
         nc.sync.dma_start(d_win[:, early:].bitcast(I32), words_of(d_words)[:, early:])
         nc.sync.dma_start(x_win[:].bitcast(I32), words_of(x_words))
         nc.sync.dma_start(rel_t[:], rel)
+        load_tab(at_tab[0])
         w_raw = sb([P, N], U32, "w_raw")
         nc.sync.dma_start(w_raw[:].bitcast(I32), words_of(w1_words))
-        load_tab(at_tab[0])
 
         def pick_keys(dealt, halves, window, move_as, size):
             for h, got in enumerate(halves):
@@ -188,11 +188,9 @@ def tile_picked_scorebias_sigmoid_po_kernel(
 
         bias0 = [sb([P, HALF], F32, "bias0_%d" % h) for h in range(2)]
         w_q = sb([P, N], U32, "w_q")
-        nc.scalar.copy(
-            w_q[:].rearrange("p (t g i) -> p g t i", t=PACK, i=PACK), w_raw[:].rearrange("p (g i t) -> p g t i", t=PACK, i=PACK)
-        )
-        nc.scalar.activation(bias0[0][:], window(0, 0, HALF), ACT.Copy)
-        nc.vector.tensor_copy(bias0[1][:], window(0, HALF, HALF))
+        deal(nc, w_q[:].bitcast(I32), w_raw[:].bitcast(I32), 0, 4)
+        for h in range(2):
+            nc.scalar.activation(bias0[h][:], window(0, h * HALF, HALF), ACT.Copy)
         first_banks = [scores(0, 0, HALF, 0)]
         score1 = [copied(1, 0, HALF, 1, at_score1)]
         first_banks.append(scores(0, HALF, HALF, 4))

@@ -99,7 +99,7 @@ def tile_picked_scorebias_sigmoid_po_kernel(
         d_sc_win = sb([P, G], U8, "d_sc_win")
         x_sc_win = sb([P, T], U8, "x_sc_win")
         d_win = sb([P, G], U32, "d_win")
-        x_win = sb([P, T], U32, "x_win")
+        x_win = placed([P, T], U32, "x_win", at_d_got)
 
         tab_rows = tab.rearrange("(p t) u -> p t u", t=PACK)
         tab_t = []
@@ -117,17 +117,14 @@ def tile_picked_scorebias_sigmoid_po_kernel(
 
         early = G // 4
         w_sc_raw = sb([P, N], U8, "w_sc_raw")
-        nc.sync.dma_start(
-            w_sc_raw[:].bitcast(I32), w1_scales[0].bitcast(I32).unsqueeze(1).to_broadcast([16, 8, N // 4])
-        )
-        w_sc_dealt = sb([P, N], U8, "w_sc_dealt")
-        deal(nc, w_sc_dealt[:], w_sc_raw[:], 0, 1)
+        nc.gpsimd.memset(w_sc_raw[:].bitcast(I32), 0)
         nc.sync.dma_start(kidx_t[:], kidx)
         nc.sync.dma_start(d_win[:, :early].bitcast(I32), words_of(d_words)[:, :early])
         load_spread(d_sc_win, d_scales)
         nc.sync.dma_start(offs_t[:], offs)
         load_spread(x_sc_win, x_scales)
         nc.sync.dma_start(d_win[:, early:].bitcast(I32), words_of(d_words)[:, early:])
+        load_spread(w_sc_raw, w1_scales)
         nc.sync.dma_start(x_win[:].bitcast(I32), words_of(x_words))
         nc.sync.dma_start(rel_t[:], rel)
         load_tab(at_tab[0])
@@ -159,6 +156,9 @@ def tile_picked_scorebias_sigmoid_po_kernel(
         x_q = [sb([P, HALF], U32, "x_q%d" % h) for h in range(2)]
         for h in range(2):
             nc.vector.tensor_copy(x_q[h][:], x_win[:].indirect(entries(offs_t, h * HALF, HALF)))
+
+        w_sc_dealt = placed([P, N], U8, "w_sc_dealt", at_d_got)
+        deal(nc, w_sc_dealt[:], w_sc_raw[:], 0, 1)
 
         last = PACK - 1
         half_bytes = 4 * HALF

@@ -205,7 +205,7 @@ def tile_picked_scorebias_sigmoid_po_kernel(
         score3 = [copied(last, h * HALF, HALF, (3, 6)[h], at_score3 + h * half_bytes) for h in range(2)]
         for h in range(2):
             add_biases(1, h * HALF, score1[h])
-        w_sc = placed([P, N], U8, "w_sc", at_score1)
+        w_sc = placed([P, N], U8, "w_sc", at_score1 + half_bytes)
         close_up(nc.sync, w_sc, w_sc_dealt, range(4))
         for number in (1, 2, 5):
             matmul(bank_tile([32, N], number, "warm_bank%d" % number)[:], w_q[:, :32], w_sc[:, :32], w_q[:], w_sc[:])
@@ -229,7 +229,8 @@ def tile_picked_scorebias_sigmoid_po_kernel(
         z = [sb([P, CHUNK, PACK], BF16, "z%d" % c) for c in chunks]
         y_late = sb([P, PACK, HALF], F32, "y_late")
         y = [sb([P, PACK, CHUNK], F32, "y0")[:], sb([P, PACK, CHUNK], F32, "y1")[:], y_late[:, :, :CHUNK], y_late[:, :, CHUNK:]]
-        y_bf = [sb([P, CHUNK, PACK], BF16, "y_bf%d" % c) for c in chunks]
+        y_bf_early = sb([P, HALF, PACK], BF16, "y_bf_early")
+        y_bf = [y_bf_early[:, :CHUNK, :], y_bf_early[:, CHUNK:, :]] + [sb([P, CHUNK, PACK], BF16, "y_bf%d" % c)[:] for c in (2, 3)]
         y_words = [sb([P, HALF], U32, "y_words%d" % h) for h in range(2)]
         y_sc = sb([P, S], U8, "y_sc")
         out_rows = out_0.rearrange("(p t) j -> p t j", t=PACK)
@@ -255,12 +256,13 @@ def tile_picked_scorebias_sigmoid_po_kernel(
                     rows = slice(t * P, (t + 1) * P)
                     matmul(banks[c, b][:, t - pair.start, :], w_q[:, rows], w_sc[:, rows], z_q[:], z_sc[:])
 
-        def planes(c):
-            h, lo = divmod(c * CHUNK, HALF)
+        def planes(first, rounded):
+            h, lo = divmod(first, HALF)
+            count = rounded.shape[1]
             nc.vector.quantize_mx(
-                out=y_words[h][:, lo : lo + CHUNK].bitcast(FP8X4),
-                scales=y_sc[:, c * CHUNK : (c + 1) * CHUNK],
-                in_=y_bf[c][:].rearrange("p j t -> p (j t)"),
+                out=y_words[h][:, lo : lo + count].bitcast(FP8X4),
+                scales=y_sc[:, first : first + count],
+                in_=rounded.rearrange("p j t -> p (j t)"),
             )
 
         def store_words(h):
@@ -281,18 +283,17 @@ def tile_picked_scorebias_sigmoid_po_kernel(
                 nc.sync.dma_start(out_rows[:, pair, c * CHUNK : (c + 1) * CHUNK], y[c][:, pair, :])
         for b, pair in enumerate(pairs):
             nc.scalar.copy(y[2][:, pair, :], banks[2, b][:])
-        interleave(nc.scalar.copy, y_bf[2][:], y[2], 4)
-        interleave(nc.vector.tensor_copy, y_bf[0][:], y[0], 4)
-        planes(0)
+        interleave(nc.scalar.copy, y_bf[2], y[2], 4)
+        interleave(nc.vector.tensor_copy, y_bf[0], y[0], 4)
+        interleave(nc.vector.tensor_copy, y_bf[1], y[1], 4)
         for b, pair in enumerate(pairs):
             nc.vector.tensor_copy(y[3][:, pair, :], banks[3, b][:])
             nc.sync.dma_start(out_rows[:, pair, HALF:], y_late[:, pair, :])
-        interleave(nc.vector.tensor_copy, y_bf[1][:], y[1], 4)
-        interleave(nc.vector.tensor_copy, y_bf[3][:], y[3], 4)
-        planes(1)
+        planes(0, y_bf_early[:])
         store_words(0)
-        planes(3)
-        planes(2)
+        interleave(nc.vector.tensor_copy, y_bf[3], y[3], 4)
+        planes(2 * CHUNK, y_bf[2])
+        planes(3 * CHUNK, y_bf[3])
         store_words(1)
         for q in range(4):
             queue = nc.sync if q % 2 else nc.scalar

from contextlib import ExitStack

import concourse.mybir as mybir

K, T, S, N, G, H, U = 512, 2048, 512, 512, 2048, 512, 1024
FLOPS = 2 * K * H * S + 2 * H * N * S

F32 = mybir.dt.float32
BF16 = mybir.dt.bfloat16
I32 = mybir.dt.int32
U32 = mybir.dt.uint32
U16 = mybir.dt.uint16
U8 = mybir.dt.uint8
FP8X4 = mybir.dt.float8_e4m3fn_x4
ACT = mybir.ActivationFunctionType
ALU = mybir.AluOpType

P = 128
PACK = 4
GROUP = 16
HALF = 256
CHUNK = 128
PAIR = 2
RUN = 8
BANKS = 8
ALIGN = 64


def words_of(dram):
    return dram[0].rearrange("p n r -> p (n r)").bitcast(I32)


def entries(list_tile, first, count):
    return list_tile[:, first // GROUP : (first + count) // GROUP]


def deal(nc, dst, src, first, size):
    run = RUN // size
    runs = slice(first // (PACK * run), (first + src.shape[1]) // (PACK * run))
    nc.vector.tensor_copy(
        dst.rearrange("p (t g i) -> p g t i", t=PACK, i=run)[:, runs],
        src.rearrange("p (g i t) -> p g t i", t=PACK, i=run),
    )


def interleave(copy, dst, src, size):
    run = RUN // size
    copy(dst.rearrange("p (g i) t -> p g t i", i=run), src.rearrange("p t (g i) -> p g t i", i=run))


def tile_picked_scorebias_sigmoid_po_kernel(
    tc, x_words, x_scales, d_words, d_scales, tab, gn, w1_words, w1_scales, offs, kidx, rel, out_0, out_1, out_2
):
    nc = tc.nc
    with ExitStack() as ctx:
        keep = ctx.enter_context(tc.tile_pool(name="keep", bufs=1))
        reuse = ctx.enter_context(tc.tile_pool(name="reuse", bufs=1))
        psum = ctx.enter_context(tc.psum_pool(name="psum", bufs=1))

        def sb(shape, dtype, name):
            return keep.tile(shape, dtype, name=name, align_bytes=ALIGN)

        def placed(shape, dtype, name, offset):
            return reuse.tile(shape, dtype, name=name, align_bytes=ALIGN, offset=offset)

        def bank_tile(shape, number, name):
            return psum.tile(shape, F32, name=name, tag="bank%d" % number)

        def load_spread(plane, dram):
            nc.sync.dma_start(plane[0:P:8, :].bitcast(I32), dram[0].bitcast(I32))

        def close_up(queue, plane, spread, rows):
            for r in rows:
                queue.dma_start(plane[r:P:32, :].bitcast(I32), spread[8 * r : P : 32, :].bitcast(I32))

        def matmul(out, lhsT, lhsT_scale, rhs, rhs_scale):
            nc.tensor.matmul_mx(
                out=out,
                lhsT=lhsT.bitcast(FP8X4),
                lhsT_scale=lhsT_scale,
                rhs=rhs.bitcast(FP8X4),
                rhs_scale=rhs_scale,
                start=True,
                stop=True,
            )

        tab_bytes = 4 * U
        at_w_raw = 0
        at_gn = 4 * N
        at_tab = [at_gn + ALIGN + 4 * tab_bytes] + [at_gn + ALIGN + t * tab_bytes for t in range(PACK - 1)]
        at_d_got = at_tab[0] + tab_bytes + ALIGN
        at_score2 = at_tab[0] - 4 * S + ALIGN
        at_score1 = at_tab[0] + ALIGN
        at_score3 = at_score1 + 4 * S

        kidx_t = keep.tile([P, H // GROUP], U16, name="kidx_t")
        offs_t = keep.tile([P, S // GROUP], U16, name="offs_t")
        rel_t = keep.tile([P, S // GROUP], U16, name="rel_t")
        d_sc_win = sb([P, G], U8, "d_sc_win")
        x_sc_win = sb([P, T], U8, "x_sc_win")
        d_win = sb([P, G], U32, "d_win")
        x_win = placed([P, T], U32, "x_win", at_d_got)

        tab_rows = tab.rearrange("(p t) u -> p t u", t=PACK)
        tab_t = []

        def load_tab(offset):
            t = len(tab_t)
            tab_t.append(placed([P, U], F32, "tab%d" % t, offset))
            nc.sync.dma_start(tab_t[t][:], tab_rows[:, t, :])

        nc.gpsimd.memset(d_sc_win[:].bitcast(I32), 0)
        nc.vector.memset(x_sc_win[:].bitcast(I32), 0)
        warm = sb([P, 2], F32, "warm")
        nc.gpsimd.memset(warm[:, 0:1], 0.0)
        nc.scalar.activation(warm[:, 1:2], warm[:, 0:1], ACT.Sigmoid)

        early = G // 4
        w_sc_raw = sb([P, N], U8, "w_sc_raw")
        nc.gpsimd.memset(w_sc_raw[:].bitcast(I32), 0)
        nc.sync.dma_start(kidx_t[:], kidx)
        nc.sync.dma_start(d_win[:, :early].bitcast(I32), words_of(d_words)[:, :early])
        load_spread(d_sc_win, d_scales)
        nc.sync.dma_start(offs_t[:], offs)
        load_spread(x_sc_win, x_scales)
        nc.sync.dma_start(d_win[:, early:].bitcast(I32), words_of(d_words)[:, early:])
        load_spread(w_sc_raw, w1_scales)
        nc.sync.dma_start(x_win[:].bitcast(I32), words_of(x_words))
        nc.sync.dma_start(rel_t[:], rel)
        load_tab(at_tab[0])
        w_raw = sb([P, N], U32, "w_raw")
        nc.sync.dma_start(w_raw[:].bitcast(I32), words_of(w1_words))

        def pick_keys(dealt, halves, window, move_as, size):
            for h, got in enumerate(halves):
                nc.vector.tensor_copy(got, window[:].indirect(entries(kidx_t, h * HALF, HALF)))
            for h, got in enumerate(halves):
                deal(nc, dealt[:].bitcast(move_as), got.bitcast(move_as), h * HALF, size)

        picked_sc = sb([P, H + S], U8, "picked_sc")
        d_sc, x_sc = picked_sc[:, :H], picked_sc[:, H:]
        d_sc_got = sb([P, H], U8, "d_sc_got")
        x_sc_got = placed([P, at_score2], U8, "x_sc_got", 0)
        nc.vector.tensor_copy(d_sc_got[:], d_sc_win[:].indirect(kidx_t[:]))
        nc.vector.tensor_copy(x_sc_got[:, :S], x_sc_win[:].indirect(offs_t[:]))
        deal(nc, d_sc, d_sc_got[:], 0, 1)
        nc.vector.tensor_copy(x_sc.bitcast(I32), x_sc_got[:, :S].bitcast(I32))
        close_up(nc.sync, picked_sc, picked_sc, range(1, 4))
        for offset in at_tab[1:]:
            load_tab(offset)
        gn_t = placed([P, PACK], F32, "gn_t", at_gn)
        nc.sync.dma_start(gn_t[:], gn.rearrange("(p t) o -> p (t o)", t=PACK))

        d_q = sb([P, H], U32, "d_q")
        pick_keys(d_q, (sb([P, HALF], U32, "d_got0")[:], sb([P, HALF], U32, "d_got1")[:]), d_win, I32, 4)
        x_q = [sb([P, HALF], U32, "x_q%d" % h) for h in range(2)]
        for h in range(2):
            nc.vector.tensor_copy(x_q[h][:], x_win[:].indirect(entries(offs_t, h * HALF, HALF)))

        w_sc_dealt = placed([P, N], U8, "w_sc_dealt", at_d_got)
        deal(nc, w_sc_dealt[:], w_sc_raw[:], 0, 1)

        last = PACK - 1
        half_bytes = 4 * HALF
        biased = {t: sb([P, S], F32, "biased%d" % t) for t in range(1, PACK)}
        biased0 = [sb([P, HALF], F32, "biased0_0"), sb([P, HALF], F32, "biased0_1")]
        sig = sb([P, 2, PACK, HALF], F32, "sig")

        def scores(t, first, count, bank_number):
            bank = bank_tile([P, count], bank_number, "score_bank%d" % bank_number)
            keys = slice(t * P, (t + 1) * P)
            for lo in range(0, count, HALF):
                cols = slice(first + lo, first + lo + HALF)
                matmul(bank[:, lo : lo + HALF], d_q[:, keys], d_sc[:, keys], x_q[cols.start // HALF][:], x_sc[:, cols])
            return bank

        def copied(t, first, count, bank_number, offset):
            tile = placed([P, count], F32, "score%d_%d" % (t, first), offset)
            nc.scalar.activation(tile[:], scores(t, first, count, bank_number)[:], ACT.Copy, scale=0.0625)
            return tile

        def window(t, first, count):
            return tab_t[t][:].indirect(entries(rel_t, first, count))

        def add_biases(t, first, score):
            count = score.shape[1]
            nc.vector.tensor_tensor(biased[t][:, first : first + count], window(t, first, count), score[:], ALU.add)

        bias0 = [sb([P, HALF], F32, "bias0_%d" % h) for h in range(2)]
        w_q = sb([P, N], U32, "w_q")
        deal(nc, w_q[:].bitcast(I32), w_raw[:].bitcast(I32), 0, 4)
        for h in range(2):
            nc.scalar.activation(bias0[h][:], window(0, h * HALF, HALF), ACT.Copy)
        first_banks = [scores(0, 0, HALF, 0)]
        score1 = [copied(1, 0, HALF, 1, at_score1)]
        first_banks.append(scores(0, HALF, HALF, 4))
        score1.append(copied(1, HALF, HALF, 5, at_score1 + half_bytes))
        for h in range(2):
            nc.vector.scalar_tensor_tensor(
                biased0[h][:], first_banks[h][:], 0.0625, bias0[h][:], ALU.mult, ALU.add
            )
        nc.scalar.activation(sig[:, 0, 0, :], biased0[0][:], ACT.Sigmoid)
        score2 = copied(2, 0, S, 2, at_score2)
        nc.scalar.activation(sig[:, 1, 0, :], biased0[1][:], ACT.Sigmoid)
        score3 = [copied(last, h * HALF, HALF, (3, 6)[h], at_score3 + h * half_bytes) for h in range(2)]
        for h in range(2):
            add_biases(1, h * HALF, score1[h])
        w_sc = placed([P, N], U8, "w_sc", at_score1 + half_bytes)
        close_up(nc.sync, w_sc, w_sc_dealt, range(4))
        for number in (1, 2, 5):
            matmul(bank_tile([32, N], number, "warm_bank%d" % number)[:], w_q[:, :32], w_sc[:, :32], w_q[:], w_sc[:])
        add_biases(2, 0, score2)
        for t in (1, 2):
            nc.scalar.activation(sig[:, :, t, :], biased[t][:].rearrange("p (h j) -> p h j", h=2), ACT.Sigmoid)
        add_biases(last, 0, score3[0])
        nc.scalar.activation(sig[:, 0, last, :], biased[last][:, :HALF], ACT.Sigmoid)
        add_biases(last, HALF, score3[1])
        z_rows = placed([P, PACK, CHUNK], BF16, "z_rows", at_score3)

        def weigh_on_scalar(t):
            nc.scalar.activation(z_rows[:, t, :], sig[:, 1, t, :CHUNK], ACT.Copy, scale=gn_t[:, t : t + 1])

        nc.scalar.activation(sig[:, 1, last, :], biased[last][:, HALF:], ACT.Sigmoid)
        for t in range(PACK):
            weigh_on_scalar(t)

        chunks = range(S // CHUNK)
        pairs = [slice(lo, lo + PAIR) for lo in range(0, PACK, PAIR)]
        z = [sb([P, CHUNK, PACK], BF16, "z%d" % c) for c in chunks]
        y_late = sb([P, PACK, HALF], F32, "y_late")
        y = [sb([P, PACK, CHUNK], F32, "y0")[:], sb([P, PACK, CHUNK], F32, "y1")[:], y_late[:, :, :CHUNK], y_late[:, :, CHUNK:]]
        y_bf_early = sb([P, HALF, PACK], BF16, "y_bf_early")
        y_bf = [y_bf_early[:, :CHUNK, :], y_bf_early[:, CHUNK:, :]] + [sb([P, CHUNK, PACK], BF16, "y_bf%d" % c)[:] for c in (2, 3)]
        y_words = [sb([P, HALF], U32, "y_words%d" % h) for h in range(2)]
        y_sc = sb([P, S], U8, "y_sc")
        out_rows = out_0.rearrange("(p t) j -> p t j", t=PACK)
        banks = {}

        def weigh(c, lo, count):
            h, first = divmod(c * CHUNK + lo, HALF)
            run = RUN // 4
            nc.vector.tensor_tensor(
                z[c][:, lo : lo + count, :].rearrange("p (g i) t -> p g t i", i=run),
                sig[:, h, :, first : first + count].rearrange("p t (g i) -> p g t i", i=run),
                gn_t[:].unsqueeze(1).unsqueeze(3).to_broadcast([P, count // run, PACK, run]),
                ALU.mult,
            )

        def product(c):
            z_q = sb([P, CHUNK], U32, "z_q%d" % c)
            z_sc = sb([P, CHUNK], U8, "z_sc%d" % c)
            nc.vector.quantize_mx(out=z_q[:].bitcast(FP8X4), scales=z_sc[:], in_=z[c][:].rearrange("p j t -> p (j t)"))
            for b, pair in enumerate(pairs):
                banks[c, b] = bank_tile([P, PAIR, CHUNK], (BANKS - 1 + len(pairs) * c + b) % BANKS, "y_bank%d_%d" % (c, b))
                for t in range(pair.start, pair.stop):
                    rows = slice(t * P, (t + 1) * P)
                    matmul(banks[c, b][:, t - pair.start, :], w_q[:, rows], w_sc[:, rows], z_q[:], z_sc[:])

        def planes(first, rounded):
            h, lo = divmod(first, HALF)
            count = rounded.shape[1]
            nc.vector.quantize_mx(
                out=y_words[h][:, lo : lo + count].bitcast(FP8X4),
                scales=y_sc[:, first : first + count],
                in_=rounded.rearrange("p j t -> p (j t)"),
            )

        def store_words(h):
            nc.sync.dma_start(words_of(out_1)[:, h * HALF : (h + 1) * HALF], y_words[h][:].bitcast(I32))

        interleave(nc.scalar.copy, z[2][:], z_rows[:], 2)
        weigh(0, 0, CHUNK)
        for ready, following in ((0, 1), (1, 3)):
            weigh(following, 0, CHUNK // 2)
            product(ready)
            weigh(following, CHUNK // 2, CHUNK // 2)
        product(2)
        product(3)

        for c in (0, 1):
            for b, pair in enumerate(pairs):
                nc.scalar.copy(y[c][:, pair, :], banks[c, b][:])
                nc.sync.dma_start(out_rows[:, pair, c * CHUNK : (c + 1) * CHUNK], y[c][:, pair, :])
        for b, pair in enumerate(pairs):
            nc.scalar.copy(y[2][:, pair, :], banks[2, b][:])
        interleave(nc.scalar.copy, y_bf[2], y[2], 4)
        interleave(nc.vector.tensor_copy, y_bf[0], y[0], 4)
        interleave(nc.vector.tensor_copy, y_bf[1], y[1], 4)
        for b, pair in enumerate(pairs):
            nc.vector.tensor_copy(y[3][:, pair, :], banks[3, b][:])
            nc.sync.dma_start(out_rows[:, pair, HALF:], y_late[:, pair, :])
        planes(0, y_bf_early[:])
        store_words(0)
        interleave(nc.vector.tensor_copy, y_bf[3], y[3], 4)
        planes(2 * CHUNK, y_bf[2])
        planes(3 * CHUNK, y_bf[3])
        store_words(1)
        for q in range(4):
            queue = nc.sync if q % 2 else nc.scalar
            queue.dma_start(out_2[0, 4 * q : 4 * q + 4, :].bitcast(I32), y_sc[32 * q : 32 * q + 4, :].bitcast(I32))
